import numpy as np
import ml_dtypes


def mxq(x, axis, fmt="e4m3"):
    dtype, down = {"e4m3": (ml_dtypes.float8_e4m3fn, 7), "e5m2": (ml_dtypes.float8_e5m2, 14)}[fmt]
    v = np.moveaxis(np.asarray(x, np.float32).astype(ml_dtypes.bfloat16).astype(np.float64), axis, -1)
    blocks = v.reshape(v.shape[:-1] + (-1, 32))
    amax = np.abs(blocks).max(-1, keepdims=True)
    byte = np.maximum(np.where(amax > 0, np.frexp(amax)[1] - 1 + 127, 0) - down, 1)
    scale = np.exp2(byte - 127.0)
    codes = (blocks / scale).astype(np.float32).astype(dtype).astype(np.float64)
    return np.moveaxis((codes * scale).reshape(v.shape), -1, axis)


WIDE = False


def mx_kscale(k):
    if not WIDE:
        return np.ones(k)
    levels = np.array([10, -10, 5, -5, 0])
    if k % 512:
        return np.exp2(np.random.permutation(np.resize(levels, k // 32))).repeat(32)
    a = np.empty((k // 512, 16))
    for p in range(k // 512):
        a[p, :8] = np.random.permutation(np.resize(levels, 8))
        for g in range(8):
            far = levels[np.abs(levels - a[p, g]) >= 10]
            a[p, g + 8] = far[np.random.randint(len(far))]
    return np.exp2(a.ravel()).repeat(32)


def f64(x):
    return np.asarray(x).astype(np.float64)


def striped(idx):
    return np.tile(idx.reshape(-1, 16).T, (8, 1)).astype(np.uint16)


def unstriped(offs):
    return offs[:16].T.reshape(-1).astype(np.int64)


E2M1 = np.array([0.0, 0.5, 1.0, 1.5, 2.0, 3.0, 4.0, 6.0, -0.0, -0.5, -1.0, -1.5, -2.0, -3.0, -4.0, -6.0])


def pack_weight(w, fmt):
    k, n = w.shape
    w = f64(np.asarray(w, np.float32).astype(ml_dtypes.bfloat16)).reshape(k // 32, 32, n)
    amax = np.abs(w).max(1)
    if fmt == "e4m3":
        byte = np.frexp(amax)[1] - 1 + 127 - 7
    else:
        mant, ex = np.frexp(amax / 6.0)
        byte = np.where(mant > 0.5, ex, ex - 1) + 127
    byte = np.clip(np.where(amax > 0, byte, 1), 1, 254)
    scaled = (w * np.exp2(127.0 - byte)[:, None, :]).reshape(k, n).astype(np.float32)
    by_word = np.ascontiguousarray(scaled.reshape(k // 512, 128, 4, n).transpose(0, 1, 3, 2))
    if fmt == "e4m3":
        words = by_word.astype(ml_dtypes.float8_e4m3fn).view(np.uint8)
    else:
        c = by_word.astype(ml_dtypes.float4_e2m1fn).view(np.uint8) & 0xF
        words = (c[..., 0::2] | (c[..., 1::2] << 4)).reshape(k // 512, 128, 2 * n)
    return np.ascontiguousarray(words), np.ascontiguousarray(byte.astype(np.uint8).reshape(k // 512, 16, n))


def unpack_weight(words, scales, fmt):
    g, _, n = scales.shape
    words = np.ascontiguousarray(words).reshape(g, 128, n, -1)
    if fmt == "e4m3":
        vals = words.view(ml_dtypes.float8_e4m3fn).astype(np.float64)
    else:
        nib = np.empty((g, 128, n, 4), np.uint8)
        nib[..., 0::2] = words & 0xF
        nib[..., 1::2] = words >> 4
        vals = E2M1[nib]
    vals = vals * np.repeat(np.exp2(scales.astype(np.float64) - 127.0), 8, axis=1)[..., None]
    return vals.transpose(0, 1, 3, 2).reshape(g * 512, n)


def gelu(v):
    return 0.5 * v * (1.0 + np.tanh(np.sqrt(2.0 / np.pi) * (v + 0.044715 * v**3)))


K, H, N, T, S, T2, P = 1536, 1024, 768, 4096, 1024, 2048, 128

def setup_inputs():
    n = np.random.standard_normal
    s = mx_kscale(K)[:, None]
    u = mx_kscale(H)[:, None]
    tab_words, tab_scales = pack_weight(n((K, T)) * s, "e4m3")
    w4_words, w4_scales = pack_weight(1.5 * n((H, N)) / np.sqrt(H) / u, "e2m1")
    return {
        "tab_words": tab_words,
        "tab_scales": tab_scales,
        "offs": striped(np.random.permutation(T)[:S]),
        "w1": (2.0 * n((K, H)) / np.sqrt(K) / s).astype(np.float32),
        "gain": (np.exp(0.3 * n(H)) * u[:, 0]).astype(np.float32),
        "w4_words": w4_words,
        "w4_scales": w4_scales,
        "wgo": np.exp(0.3 * n((P, S))).astype(np.float32),
        "offs2": striped(np.random.permutation(T2)[:S]),
    }

def reference(tab_words, tab_scales, offs, w1, gain, w4_words, w4_scales, wgo, offs2):
    v = unpack_weight(tab_words, tab_scales, "e4m3")[:, unstriped(offs)]
    w1q = mxq(f64(w1), 0, "e4m3")
    x = np.maximum(w1q.T @ v, 0.0)
    h = np.log(1.0 + x) * f64(gain)[:, None]
    hq = mxq(h, 0, "e4m3")
    w4 = unpack_weight(w4_words, w4_scales, "e2m1")
    y = np.maximum(w4.T @ hq, 0.0)
    out = np.zeros((N, T2))
    out[:, unstriped(offs2)] = np.tile(f64(wgo), (N // P, 1)) * y
    return out

@@ -1,0 +1,210 @@
+from contextlib import ExitStack
+
+import concourse.mybir as mybir
+
+K, H, N, T, S, T2, P = 1536, 1024, 768, 4096, 1024, 2048, 128
+FLOPS = 2 * K * H * S + 2 * H * N * S
+
+F32 = mybir.dt.float32
+BF16 = mybir.dt.bfloat16
+I32 = mybir.dt.int32
+U32 = mybir.dt.uint32
+U16 = mybir.dt.uint16
+U8 = mybir.dt.uint8
+FP8X4 = mybir.dt.float8_e4m3fn_x4
+FP4X4 = mybir.dt.float4_e2m1fn_x4
+ACT = mybir.ActivationFunctionType
+ALU = mybir.AluOpType
+
+PACK = 4
+PASS = P * PACK
+KA = K // PASS
+HB = H // PASS
+NT = N // P
+HALF = 512
+SH = S // HALF
+LIST = 16
+
+
+def tile_list_posting_term_expansion_kernel(
+    tc, tab_words, tab_scales, offs, w1, gain, w4_words, w4_scales, wgo, offs2, out
+):
+    nc = tc.nc
+    with ExitStack() as ctx:
+        keep = ctx.enter_context(tc.tile_pool(name="keep", bufs=1))
+        stage = ctx.enter_context(tc.tile_pool(name="stage", bufs=2))
+        psum = ctx.enter_context(tc.psum_pool(name="psum", bufs=1))
+
+        picks = keep.tile([P, S // LIST], U16, name="picks")
+        places = keep.tile([P, S // LIST], U16, name="places")
+        tab_w = [keep.tile([P, T], I32, name=f"tab_w{a}", align_bytes=64) for a in range(KA)]
+        tab_s = keep.tile([P, T // 4], I32, name="tab_s", align_bytes=64)
+        v_w = [keep.tile([P, S], U32, name=f"v_w{a}", align_bytes=64) for a in range(KA)]
+        v_s = keep.tile([P, S], U8, name="v_s", align_bytes=64)
+        w4_w = keep.tile([P, HB, 2 * N // 4], I32, name="w4_w", align_bytes=64)
+        w4_s = keep.tile([P, HB, N // 4], I32, name="w4_s", align_bytes=64)
+        gains = keep.tile([P, HB, PACK], F32, name="gains")
+        weights = keep.tile([P, S], F32, name="weights")
+        cache = [keep.tile([P, T2], F32, name=f"cache{n}") for n in range(NT)]
+        one = keep.tile([P, 1], F32, name="one")
+        warm = keep.tile([P, 1], F32, name="warm")
+
+        nc.vector.memset(tab_s[:], 0)
+        nc.vector.memset(one[:], 1.0)
+        nc.scalar.activation(warm[:], one[:], ACT.Ln)
+        nc.vector.memset(w4_s[:], 0)
+        for n in range(NT):
+            nc.vector.memset(cache[n][:], 0.0)
+
+        def load_table(a):
+            nc.sync.dma_start(tab_w[a][:], tab_words[a].rearrange("p t i -> p (t i)").bitcast(I32))
+
+        load_table(0)
+        nc.sync.dma_start(picks[:], offs)
+        for q in range(4):
+            nc.sync.dma_start(
+                tab_s[32 * q : 32 * q + 4 * KA, :], tab_scales[:, 4 * q : 4 * q + 4, :].bitcast(I32)
+            )
+        load_table(1)
+        load_table(2)
+
+        raw = {}
+        for b in range(HB):
+            for a in range(KA):
+                raw[b, a] = stage.tile([P, PACK, PASS], F32, name="raw", bufs=4)
+                nc.sync.dma_start(
+                    raw[b, a][:],
+                    w1[PASS * a : PASS * (a + 1), PASS * b : PASS * (b + 1)].rearrange("(p j) c -> p j c", j=PACK),
+                )
+            if b == 0:
+                nc.sync.dma_start(gains[:], gain.rearrange("(b p t) -> p b t", b=HB, t=PACK))
+        nc.sync.dma_start(w4_w[:], w4_words.rearrange("b p c -> p b c").bitcast(I32))
+        for q in range(4):
+            nc.sync.dma_start(
+                w4_s[32 * q : 32 * q + 4, :, :],
+                w4_scales[:, 4 * q : 4 * q + 4, :].rearrange("b r n -> r b n").bitcast(I32),
+            )
+        nc.sync.dma_start(weights[:], wgo)
+        nc.sync.dma_start(places[:], offs2)
+
+        nc.vector.tensor_copy(v_w[0][:], tab_w[0][:].bitcast(U32).indirect(picks[:]))
+        nc.vector.tensor_copy(v_s[:], tab_s[:].bitcast(U8).indirect(picks[:]))
+        for a in range(1, KA):
+            nc.vector.tensor_copy(v_w[a][:], tab_w[a][:].bitcast(U32).indirect(picks[:]))
+
+        w1_w, w1_s = {}, {}
+
+        def quantise_w1(b, a, scalar_share):
+            grouped = stage.tile([P, PACK * PASS], BF16, name="grouped", align_bytes=64)
+            dst = grouped[:].rearrange("p (t m j) -> p m j t", t=PACK, j=PACK)
+            src = raw[b, a][:].rearrange("p j (m t) -> p m j t", t=PACK)
+            if scalar_share > 0:
+                nc.scalar.activation(dst[:, :scalar_share], src[:, :scalar_share], ACT.Copy)
+            if scalar_share < P:
+                nc.vector.tensor_copy(dst[:, scalar_share:], src[:, scalar_share:])
+            w1_w[b, a] = keep.tile([P, PASS], U32, name=f"w1_w{b}{a}", align_bytes=64)
+            w1_s[b, a] = keep.tile([P, PASS], U8, name=f"w1_s{b}{a}", align_bytes=64)
+            nc.vector.quantize_mx(w1_w[b, a][:].bitcast(FP8X4), w1_s[b, a][:], grouped[:])
+
+        def bank(i):
+            return psum.tile([P, HALF], F32, name=f"bank{i}")
+
+        x_sum = {}
+
+        def first_product(b, h, a):
+            cols = slice(HALF * h, HALF * (h + 1))
+            for t in range(PACK):
+                if a == 0:
+                    x_sum[b, h, t] = bank(PACK * h + t)
+                rows = slice(P * t, P * (t + 1))
+                nc.tensor.matmul_mx(
+                    x_sum[b, h, t][:],
+                    lhsT=w1_w[b, a][:, rows].bitcast(FP8X4),
+                    lhsT_scale=w1_s[b, a][:, rows],
+                    rhs=v_w[a][:, cols].bitcast(FP8X4),
+                    rhs_scale=v_s[4 * a : P, cols],
+                    start=(a == 0),
+                    stop=(a == KA - 1),
+                )
+
+        h_w, h_s = {}, {}
+
+        def features(b, h):
+            x = stage.tile([P, PACK, HALF], F32, name="x")
+            for t in range(PACK):
+                nc.scalar.activation(x[:, t, :], x_sum[b, h, t][:], ACT.Relu)
+                if t > 0:
+                    nc.scalar.activation(x[:, t - 1, :], x[:, t - 1, :], ACT.Ln, bias=1.0)
+            nc.scalar.activation(x[:, PACK - 1, :], x[:, PACK - 1, :], ACT.Ln, bias=1.0)
+            feat = stage.tile([P, PACK * HALF], BF16, name="feat", align_bytes=64)
+            if h == 0:
+                nc.vector.tensor_tensor(
+                    feat[:].rearrange("p (c i t) -> p c t i", i=4, t=PACK),
+                    x[:].rearrange("p t (c i) -> p c t i", i=4),
+                    gains[:, b, :].unsqueeze(1).unsqueeze(3).to_broadcast([P, HALF // 4, PACK, 4]),
+                    ALU.mult,
+                )
+            else:
+                planes = stage.tile([P, PACK, HALF], BF16, name="planes")
+                for t in range(PACK):
+                    nc.scalar.activation(planes[:, t, :], x[:, t, :], ACT.Copy, scale=gains[:, b, t : t + 1])
+                nc.scalar.copy(
+                    feat[:].rearrange("p (c i t) -> p c t i", i=4, t=PACK),
+                    planes[:].rearrange("p t (c i) -> p c t i", i=4),
+                )
+            h_w[b, h] = keep.tile([P, HALF], U32, name=f"h_w{b}{h}", align_bytes=64)
+            h_s[b, h] = keep.tile([P, HALF], U8, name=f"h_s{b}{h}", align_bytes=64)
+            nc.vector.quantize_mx(h_w[b, h][:].bitcast(FP8X4), h_s[b, h][:], feat[:])
+
+        w4_bytes = w4_w[:].bitcast(U8)
+        w4_scale_bytes = w4_s[:].bitcast(U8)
+
+        def weighted(h, n):
+            y_sum = bank(PACK * h + n % PACK)
+            for b in range(HB):
+                nc.tensor.matmul_mx(
+                    y_sum[:],
+                    lhsT=w4_bytes[:, b, 2 * P * n : 2 * P * (n + 1)].bitcast(FP4X4),
+                    lhsT_scale=w4_scale_bytes[:, b, P * n : P * (n + 1)],
+                    rhs=h_w[b, h][:].bitcast(FP8X4),
+                    rhs_scale=h_s[b, h][:],
+                    start=(b == 0),
+                    stop=(b == HB - 1),
+                )
+            y = stage.tile([P, HALF], F32, name="y", bufs=3)
+            nc.vector.scalar_tensor_tensor(
+                y[:], y_sum[:], 0.0, weights[:, HALF * h : HALF * (h + 1)], ALU.max, ALU.mult
+            )
+            return y
+
+        def place(h, n, y):
+            entries = places[:, HALF // LIST * h : HALF // LIST * (h + 1)]
+            nc.vector.tensor_copy(cache[n][:].indirect(entries), y[:])
+            if h == SH - 1:
+                nc.sync.dma_start(out[P * n : P * (n + 1), :], cache[n][:])
+
+        def expansion(h):
+            held = None
+            for n in range(NT):
+                y = weighted(h, n)
+                if held is not None:
+                    place(h, n - 1, held)
+                held = y
+            place(h, NT - 1, held)
+
+        for a in range(KA):
+            quantise_w1(0, a, P if a < KA - 1 else 48)
+            for h in range(SH):
+                first_product(0, h, a)
+        for a in range(KA):
+            quantise_w1(1, a, 0)
+        features(0, 0)
+        for a in range(KA):
+            first_product(1, 0, a)
+        features(1, 0)
+        features(0, 1)
+        for a in range(KA):
+            first_product(1, 1, a)
+        features(1, 1)
+        expansion(0)
+        expansion(1)

@@ -21,8 +21,8 @@ PASS = P * PACK
 KA = K // PASS
 HB = H // PASS
 NT = N // P
-HALF = 512
-SH = S // HALF
+BANK = 512
+PIECES = [(0, 256), (256, 384), (640, 384)]
 LIST = 16
 
 
@@ -54,7 +54,7 @@ def tile_list_posting_term_expansion_kernel(
         nc.scalar.activation(warm[:], one[:], ACT.Ln)
         nc.vector.memset(w4_s[:], 0)
         for n in range(NT):
-            nc.vector.memset(cache[n][:], 0.0)
+            nc.gpsimd.memset(cache[n][:], 0.0)
 
         def load_table(a):
             nc.sync.dma_start(tab_w[a][:], tab_words[a].rearrange("p t i -> p (t i)").bitcast(I32))
@@ -71,11 +71,13 @@ def tile_list_posting_term_expansion_kernel(
         raw = {}
         for b in range(HB):
             for a in range(KA):
-                raw[b, a] = stage.tile([P, PACK, PASS], F32, name="raw", bufs=4)
-                nc.sync.dma_start(
-                    raw[b, a][:],
-                    w1[PASS * a : PASS * (a + 1), PASS * b : PASS * (b + 1)].rearrange("(p j) c -> p j c", j=PACK),
-                )
+                raw[b, a] = stage.tile([P, PACK, PASS], F32, name="raw", bufs=3)
+                block = w1[PASS * a : PASS * (a + 1), PASS * b : PASS * (b + 1)].rearrange("(p j) c -> p j c", j=PACK)
+                if (b, a) == (HB - 1, KA - 1):
+                    for c0 in range(0, PASS, PASS // 2):
+                        nc.sync.dma_start(raw[b, a][:, :, c0 : c0 + PASS // 2], block[:, :, c0 : c0 + PASS // 2])
+                else:
+                    nc.sync.dma_start(raw[b, a][:], block)
             if b == 0:
                 nc.sync.dma_start(gains[:], gain.rearrange("(b p t) -> p b t", b=HB, t=PACK))
         nc.sync.dma_start(w4_w[:], w4_words.rearrange("b p c -> p b c").bitcast(I32))
@@ -94,117 +96,151 @@ def tile_list_posting_term_expansion_kernel(
 
         w1_w, w1_s = {}, {}
 
-        def quantise_w1(b, a, scalar_share):
+        def quantise_w1(b, a, shares, quantise_width):
             grouped = stage.tile([P, PACK * PASS], BF16, name="grouped", align_bytes=64)
             dst = grouped[:].rearrange("p (t m j) -> p m j t", t=PACK, j=PACK)
             src = raw[b, a][:].rearrange("p j (m t) -> p m j t", t=PACK)
-            if scalar_share > 0:
-                nc.scalar.activation(dst[:, :scalar_share], src[:, :scalar_share], ACT.Copy)
-            if scalar_share < P:
-                nc.vector.tensor_copy(dst[:, scalar_share:], src[:, scalar_share:])
+            for engine, m0, m1 in shares:
+                if engine == "scalar":
+                    nc.scalar.activation(dst[:, m0:m1], src[:, m0:m1], ACT.Copy)
+                else:
+                    nc.vector.tensor_copy(dst[:, m0:m1], src[:, m0:m1])
             w1_w[b, a] = keep.tile([P, PASS], U32, name=f"w1_w{b}{a}", align_bytes=64)
             w1_s[b, a] = keep.tile([P, PASS], U8, name=f"w1_s{b}{a}", align_bytes=64)
-            nc.vector.quantize_mx(w1_w[b, a][:].bitcast(FP8X4), w1_s[b, a][:], grouped[:])
-
-        def bank(i):
-            return psum.tile([P, HALF], F32, name=f"bank{i}")
-
-        x_sum = {}
-
-        def first_product(b, h, a):
-            cols = slice(HALF * h, HALF * (h + 1))
-            for t in range(PACK):
-                if a == 0:
-                    x_sum[b, h, t] = bank(PACK * h + t)
-                rows = slice(P * t, P * (t + 1))
-                nc.tensor.matmul_mx(
-                    x_sum[b, h, t][:],
-                    lhsT=w1_w[b, a][:, rows].bitcast(FP8X4),
-                    lhsT_scale=w1_s[b, a][:, rows],
-                    rhs=v_w[a][:, cols].bitcast(FP8X4),
-                    rhs_scale=v_s[4 * a : P, cols],
-                    start=(a == 0),
-                    stop=(a == KA - 1),
+            for c0 in range(0, PASS, quantise_width):
+                nc.vector.quantize_mx(
+                    w1_w[b, a][:, c0 : c0 + quantise_width].bitcast(FP8X4),
+                    w1_s[b, a][:, c0 : c0 + quantise_width],
+                    grouped[:, PACK * c0 : PACK * (c0 + quantise_width)],
                 )
 
-        h_w, h_s = {}, {}
+        def bank(i):
+            return psum.tile([P, BANK], F32, name=f"bank{i}")
 
-        def features(b, h):
-            x = stage.tile([P, PACK, HALF], F32, name="x")
+        def runs(width):
+            return [(0, 256)] if width == 256 else [(0, 256), (256, 384)]
+
+        def first_pass(x_sum, b, a, t, c0, c1, start):
+            rows = slice(P * t, P * (t + 1))
+            cols = slice(start + c0, start + c1)
+            nc.tensor.matmul_mx(
+                x_sum[:, c0:c1],
+                lhsT=w1_w[b, a][:, rows].bitcast(FP8X4),
+                lhsT_scale=w1_s[b, a][:, rows],
+                rhs=v_w[a][:, cols].bitcast(FP8X4),
+                rhs_scale=v_s[4 * a : P, cols],
+                start=(a == 0),
+                stop=(a == KA - 1),
+            )
+
+        def first_product(b, piece, t, bank_index):
+            start, width = PIECES[piece]
+            x_sum = bank(bank_index)
+            for c0, c1 in runs(width):
+                for a in range(KA):
+                    first_pass(x_sum, b, a, t, c0, c1, start)
+            return x_sum
+
+        def saturate(sum_of, piece):
+            width = PIECES[piece][1]
+            x = stage.tile([P, PACK, width], F32, name="x", bufs=4)
             for t in range(PACK):
-                nc.scalar.activation(x[:, t, :], x_sum[b, h, t][:], ACT.Relu)
+                nc.scalar.activation(x[:, t, :], sum_of(t)[:, :width], ACT.Relu)
                 if t > 0:
                     nc.scalar.activation(x[:, t - 1, :], x[:, t - 1, :], ACT.Ln, bias=1.0)
             nc.scalar.activation(x[:, PACK - 1, :], x[:, PACK - 1, :], ACT.Ln, bias=1.0)
-            feat = stage.tile([P, PACK * HALF], BF16, name="feat", align_bytes=64)
-            if h == 0:
-                nc.vector.tensor_tensor(
-                    feat[:].rearrange("p (c i t) -> p c t i", i=4, t=PACK),
-                    x[:].rearrange("p t (c i) -> p c t i", i=4),
-                    gains[:, b, :].unsqueeze(1).unsqueeze(3).to_broadcast([P, HALF // 4, PACK, 4]),
-                    ALU.mult,
-                )
-            else:
-                planes = stage.tile([P, PACK, HALF], BF16, name="planes")
+            return x
+
+        def features(b, piece, banks):
+            return saturate(lambda t: first_product(b, piece, t, banks[t]), piece)
+
+        h_w, h_s = {}, {}
+
+        def quantise_h(x, b, piece, engine):
+            width = PIECES[piece][1]
+            feat = stage.tile([P, PACK * width], BF16, name="feat", align_bytes=64, bufs=3)
+            h_w[b, piece] = keep.tile([P, width], U32, name=f"h_w{b}{piece}", align_bytes=64)
+            h_s[b, piece] = keep.tile([P, width], U8, name=f"h_s{b}{piece}", align_bytes=64)
+            if engine == "scalar":
+                planes = keep.tile([P, PACK, width], BF16, name=f"planes{b}{piece}")
                 for t in range(PACK):
                     nc.scalar.activation(planes[:, t, :], x[:, t, :], ACT.Copy, scale=gains[:, b, t : t + 1])
-                nc.scalar.copy(
-                    feat[:].rearrange("p (c i t) -> p c t i", i=4, t=PACK),
-                    planes[:].rearrange("p t (c i) -> p c t i", i=4),
+            for c0, c1 in runs(width):
+                dst = feat[:, PACK * c0 : PACK * c1].rearrange("p (c i t) -> p c t i", i=4, t=PACK)
+                if engine == "scalar":
+                    nc.scalar.copy(dst, planes[:, :, c0:c1].rearrange("p t (c i) -> p c t i", i=4))
+                else:
+                    nc.vector.tensor_tensor(
+                        dst,
+                        x[:, :, c0:c1].rearrange("p t (c i) -> p c t i", i=4),
+                        gains[:, b, :].unsqueeze(1).unsqueeze(3).to_broadcast([P, (c1 - c0) // 4, PACK, 4]),
+                        ALU.mult,
+                    )
+            for c0, c1 in runs(width):
+                nc.vector.quantize_mx(
+                    h_w[b, piece][:, c0:c1].bitcast(FP8X4), h_s[b, piece][:, c0:c1], feat[:, PACK * c0 : PACK * c1]
                 )
-            h_w[b, h] = keep.tile([P, HALF], U32, name=f"h_w{b}{h}", align_bytes=64)
-            h_s[b, h] = keep.tile([P, HALF], U8, name=f"h_s{b}{h}", align_bytes=64)
-            nc.vector.quantize_mx(h_w[b, h][:].bitcast(FP8X4), h_s[b, h][:], feat[:])
 
         w4_bytes = w4_w[:].bitcast(U8)
         w4_scale_bytes = w4_s[:].bitcast(U8)
 
-        def weighted(h, n):
-            y_sum = bank(PACK * h + n % PACK)
-            for b in range(HB):
-                nc.tensor.matmul_mx(
-                    y_sum[:],
-                    lhsT=w4_bytes[:, b, 2 * P * n : 2 * P * (n + 1)].bitcast(FP4X4),
-                    lhsT_scale=w4_scale_bytes[:, b, P * n : P * (n + 1)],
-                    rhs=h_w[b, h][:].bitcast(FP8X4),
-                    rhs_scale=h_s[b, h][:],
-                    start=(b == 0),
-                    stop=(b == HB - 1),
+        def expansion(piece, tiles, held=None):
+            start, width = PIECES[piece]
+            entries = places[:, start // LIST : (start + width) // LIST]
+            if held is not None:
+                late = keep.tile([P, len(tiles), width], F32, name=held)
+            for n in tiles:
+                y_sum = bank(6 + n % 2)
+                for c0 in range(0, width, P):
+                    for b in range(HB):
+                        nc.tensor.matmul_mx(
+                            y_sum[:, c0 : c0 + P],
+                            lhsT=w4_bytes[:, b, 2 * P * n : 2 * P * (n + 1)].bitcast(FP4X4),
+                            lhsT_scale=w4_scale_bytes[:, b, P * n : P * (n + 1)],
+                            rhs=h_w[b, piece][:, c0 : c0 + P].bitcast(FP8X4),
+                            rhs_scale=h_s[b, piece][:, c0 : c0 + P],
+                            start=(b == 0),
+                            stop=(b == HB - 1),
+                        )
+                if held is None:
+                    y = stage.tile([P, width], F32, name="y", bufs=8)[:]
+                else:
+                    y = late[:, n - tiles[0], :]
+                nc.scalar.activation(y, y_sum[:, :width], ACT.Relu)
+                nc.vector.tensor_tensor(
+                    cache[n][:].indirect(entries), y, weights[:, start : start + width], ALU.mult
                 )
-            y = stage.tile([P, HALF], F32, name="y", bufs=3)
-            nc.vector.scalar_tensor_tensor(
-                y[:], y_sum[:], 0.0, weights[:, HALF * h : HALF * (h + 1)], ALU.max, ALU.mult
-            )
-            return y
+                if piece == len(PIECES) - 1:
+                    nc.sync.dma_start(out[P * n : P * (n + 1), :], cache[n][:])
 
-        def place(h, n, y):
-            entries = places[:, HALF // LIST * h : HALF // LIST * (h + 1)]
-            nc.vector.tensor_copy(cache[n][:].indirect(entries), y[:])
-            if h == SH - 1:
-                nc.sync.dma_start(out[P * n : P * (n + 1), :], cache[n][:])
+        first_width = PIECES[0][1]
+        both = [("scalar", 0, 48), ("vector", 48, P)]
 
-        def expansion(h):
-            held = None
-            for n in range(NT):
-                y = weighted(h, n)
-                if held is not None:
-                    place(h, n - 1, held)
-                held = y
-            place(h, NT - 1, held)
+        sums = [bank(t) for t in range(PACK)]
+        for a in range(KA):
+            quantise_w1(0, a, both, PASS)
+            for t in range(PACK):
+                first_pass(sums[t], 0, a, t, 0, first_width, 0)
+        x00 = saturate(lambda t: sums[t], 0)
+        x01 = features(0, 1, [4, 5, 6, 7])
 
+        sums = [bank(t) for t in range(PACK)]
         for a in range(KA):
-            quantise_w1(0, a, P if a < KA - 1 else 48)
-            for h in range(SH):
-                first_product(0, h, a)
-        for a in range(KA):
-            quantise_w1(1, a, 0)
-        features(0, 0)
-        for a in range(KA):
-            first_product(1, 0, a)
-        features(1, 0)
-        features(0, 1)
-        for a in range(KA):
-            first_product(1, 1, a)
-        features(1, 1)
-        expansion(0)
-        expansion(1)
+            if a < KA - 1:
+                quantise_w1(1, a, [("vector", 0, P)], PASS)
+            else:
+                quantise_w1(1, a, [("vector", 0, 64), ("vector", 64, 104), ("scalar", 104, P)], P)
+            for t in range(PACK):
+                first_pass(sums[t], 1, a, t, 0, first_width, 0)
+        x10 = saturate(lambda t: sums[t], 0)
+        quantise_h(x10, 1, 0, "vector")
+        quantise_h(x00, 0, 0, "vector")
+        quantise_h(x01, 0, 1, "vector")
+        expansion(0, [0, 1, 2, 3])
+        quantise_h(features(1, 1, [0, 1, 2, 3]), 1, 1, "scalar")
+        expansion(0, [4, 5], "planes11")
+        expansion(1, [0, 1, 2, 3])
+        quantise_h(features(0, 2, [4, 5, 4, 5]), 0, 2, "scalar")
+        quantise_h(features(1, 2, [0, 1, 2, 3]), 1, 2, "scalar")
+        expansion(1, [4, 5], "planes12")
+        expansion(2, range(NT))

@@ -54,7 +54,7 @@ def tile_list_posting_term_expansion_kernel(
         nc.scalar.activation(warm[:], one[:], ACT.Ln)
         nc.vector.memset(w4_s[:], 0)
         for n in range(NT):
-            nc.gpsimd.memset(cache[n][:], 0.0)
+            (nc.vector if n < 3 else nc.gpsimd).memset(cache[n][:], 0.0)
 
         def load_table(a):
             nc.sync.dma_start(tab_w[a][:], tab_words[a].rearrange("p t i -> p (t i)").bitcast(I32))
@@ -65,21 +65,25 @@ def tile_list_posting_term_expansion_kernel(
             nc.sync.dma_start(
                 tab_s[32 * q : 32 * q + 4 * KA, :], tab_scales[:, 4 * q : 4 * q + 4, :].bitcast(I32)
             )
-        load_table(1)
-        load_table(2)
+        nc.sync.dma_start(gains[:], gain.rearrange("(b p t) -> p b t", b=HB, t=PACK))
 
         raw = {}
-        for b in range(HB):
-            for a in range(KA):
-                raw[b, a] = stage.tile([P, PACK, PASS], F32, name="raw", bufs=3)
-                block = w1[PASS * a : PASS * (a + 1), PASS * b : PASS * (b + 1)].rearrange("(p j) c -> p j c", j=PACK)
-                if (b, a) == (HB - 1, KA - 1):
-                    for c0 in range(0, PASS, PASS // 2):
-                        nc.sync.dma_start(raw[b, a][:, :, c0 : c0 + PASS // 2], block[:, :, c0 : c0 + PASS // 2])
-                else:
-                    nc.sync.dma_start(raw[b, a][:], block)
-            if b == 0:
-                nc.sync.dma_start(gains[:], gain.rearrange("(b p t) -> p b t", b=HB, t=PACK))
+
+        def load_w1(b, a, parts=1):
+            raw[b, a] = stage.tile([P, PACK, PASS], F32, name="raw", bufs=3)
+            block = w1[PASS * a : PASS * (a + 1), PASS * b : PASS * (b + 1)].rearrange("(p j) c -> p j c", j=PACK)
+            for c0 in range(0, PASS, PASS // parts):
+                cols = slice(c0, c0 + PASS // parts)
+                nc.sync.dma_start(raw[b, a][:, :, cols], block[:, :, cols])
+
+        load_w1(1, 0)
+        load_w1(0, 0)
+        load_table(1)
+        load_w1(0, 1)
+        load_table(2)
+        load_w1(0, 2)
+        load_w1(1, 1)
+        load_w1(1, 2, parts=2)
         nc.sync.dma_start(w4_w[:], w4_words.rearrange("b p c -> p b c").bitcast(I32))
         for q in range(4):
             nc.sync.dma_start(
@@ -98,8 +102,8 @@ def tile_list_posting_term_expansion_kernel(
 
         def quantise_w1(b, a, shares, quantise_width):
             grouped = stage.tile([P, PACK * PASS], BF16, name="grouped", align_bytes=64)
-            dst = grouped[:].rearrange("p (t m j) -> p m j t", t=PACK, j=PACK)
-            src = raw[b, a][:].rearrange("p j (m t) -> p m j t", t=PACK)
+            dst = grouped[:].rearrange("p (t m j) -> p m t j", t=PACK, j=PACK)
+            src = raw[b, a][:].rearrange("p j (m t) -> p m t j", t=PACK)
             for engine, m0, m1 in shares:
                 if engine == "scalar":
                     nc.scalar.activation(dst[:, m0:m1], src[:, m0:m1], ACT.Copy)
@@ -141,11 +145,14 @@ def tile_list_posting_term_expansion_kernel(
                     first_pass(x_sum, b, a, t, c0, c1, start)
             return x_sum
 
-        def saturate(sum_of, piece):
+        def saturate(sum_of, piece, vector_planes=()):
             width = PIECES[piece][1]
             x = stage.tile([P, PACK, width], F32, name="x", bufs=4)
             for t in range(PACK):
-                nc.scalar.activation(x[:, t, :], sum_of(t)[:, :width], ACT.Relu)
+                if t in vector_planes:
+                    nc.vector.tensor_scalar_max(x[:, t, :], sum_of(t)[:, :width], 0.0)
+                else:
+                    nc.scalar.activation(x[:, t, :], sum_of(t)[:, :width], ACT.Relu)
                 if t > 0:
                     nc.scalar.activation(x[:, t - 1, :], x[:, t - 1, :], ACT.Ln, bias=1.0)
             nc.scalar.activation(x[:, PACK - 1, :], x[:, PACK - 1, :], ACT.Ln, bias=1.0)
@@ -156,9 +163,9 @@ def tile_list_posting_term_expansion_kernel(
 
         h_w, h_s = {}, {}
 
-        def quantise_h(x, b, piece, engine):
+        def quantise_h(x, b, piece, engine, slot):
             width = PIECES[piece][1]
-            feat = stage.tile([P, PACK * width], BF16, name="feat", align_bytes=64, bufs=3)
+            feat = keep.tile([P, PACK * width], BF16, name=f"feat{slot}", align_bytes=64)
             h_w[b, piece] = keep.tile([P, width], U32, name=f"h_w{b}{piece}", align_bytes=64)
             h_s[b, piece] = keep.tile([P, width], U8, name=f"h_s{b}{piece}", align_bytes=64)
             if engine == "scalar":
@@ -166,14 +173,14 @@ def tile_list_posting_term_expansion_kernel(
                 for t in range(PACK):
                     nc.scalar.activation(planes[:, t, :], x[:, t, :], ACT.Copy, scale=gains[:, b, t : t + 1])
             for c0, c1 in runs(width):
-                dst = feat[:, PACK * c0 : PACK * c1].rearrange("p (c i t) -> p c t i", i=4, t=PACK)
+                dst = feat[:, PACK * c0 : PACK * c1].rearrange("p (c t) -> p c t", t=PACK)
                 if engine == "scalar":
-                    nc.scalar.copy(dst, planes[:, :, c0:c1].rearrange("p t (c i) -> p c t i", i=4))
+                    nc.scalar.copy(dst, planes[:, :, c0:c1].rearrange("p t c -> p c t"))
                 else:
                     nc.vector.tensor_tensor(
                         dst,
-                        x[:, :, c0:c1].rearrange("p t (c i) -> p c t i", i=4),
-                        gains[:, b, :].unsqueeze(1).unsqueeze(3).to_broadcast([P, (c1 - c0) // 4, PACK, 4]),
+                        x[:, :, c0:c1].rearrange("p t c -> p c t"),
+                        gains[:, b, :].unsqueeze(1).to_broadcast([P, c1 - c0, PACK]),
                         ALU.mult,
                     )
             for c0, c1 in runs(width):
@@ -214,33 +221,31 @@ def tile_list_posting_term_expansion_kernel(
                     nc.sync.dma_start(out[P * n : P * (n + 1), :], cache[n][:])
 
         first_width = PIECES[0][1]
-        both = [("scalar", 0, 48), ("vector", 48, P)]
 
+        quantise_w1(1, 0, [("scalar", 0, P)], PASS)
         sums = [bank(t) for t in range(PACK)]
         for a in range(KA):
-            quantise_w1(0, a, both, PASS)
+            quantise_w1(0, a, [("scalar", 0, P)] if a < KA - 1 else [("scalar", 0, 44), ("vector", 44, P)], PASS)
             for t in range(PACK):
                 first_pass(sums[t], 0, a, t, 0, first_width, 0)
         x00 = saturate(lambda t: sums[t], 0)
-        x01 = features(0, 1, [4, 5, 6, 7])
 
-        sums = [bank(t) for t in range(PACK)]
+        quantise_w1(1, 1, [("vector", 0, P)], PASS)
+        quantise_w1(1, 2, [("vector", 0, 64), ("vector", 64, 106), ("scalar", 106, P)], P)
+        sums = [bank(PACK + t) for t in range(PACK)]
         for a in range(KA):
-            if a < KA - 1:
-                quantise_w1(1, a, [("vector", 0, P)], PASS)
-            else:
-                quantise_w1(1, a, [("vector", 0, 64), ("vector", 64, 104), ("scalar", 104, P)], P)
             for t in range(PACK):
                 first_pass(sums[t], 1, a, t, 0, first_width, 0)
-        x10 = saturate(lambda t: sums[t], 0)
-        quantise_h(x10, 1, 0, "vector")
-        quantise_h(x00, 0, 0, "vector")
-        quantise_h(x01, 0, 1, "vector")
+        x10 = saturate(lambda t: sums[t], 0, (1, 3))
+        x01 = features(0, 1, [0, 1, 2, 3])
+        quantise_h(x10, 1, 0, "vector", 0)
+        quantise_h(x00, 0, 0, "vector", 1)
+        quantise_h(x01, 0, 1, "vector", 0)
         expansion(0, [0, 1, 2, 3])
-        quantise_h(features(1, 1, [0, 1, 2, 3]), 1, 1, "scalar")
+        quantise_h(features(1, 1, [4, 5, 4, 5]), 1, 1, "scalar", 1)
         expansion(0, [4, 5], "planes11")
-        expansion(1, [0, 1, 2, 3])
-        quantise_h(features(0, 2, [4, 5, 4, 5]), 0, 2, "scalar")
-        quantise_h(features(1, 2, [0, 1, 2, 3]), 1, 2, "scalar")
-        expansion(1, [4, 5], "planes12")
+        expansion(1, [0, 1, 2, 3, 4])
+        quantise_h(features(0, 2, [0, 1, 2, 3]), 0, 2, "scalar", 0)
+        quantise_h(features(1, 2, [0, 1, 2, 3]), 1, 2, "scalar", 1)
+        expansion(1, [5], "planes12")
         expansion(2, range(NT))

@@ -44,6 +44,7 @@ def tile_list_posting_term_expansion_kernel(
         w4_w = keep.tile([P, HB, 2 * N // 4], I32, name="w4_w", align_bytes=64)
         w4_s = keep.tile([P, HB, N // 4], I32, name="w4_s", align_bytes=64)
         gains = keep.tile([P, HB, PACK], F32, name="gains")
+        gain_rows = [keep.tile([P, P, PACK], F32, name=f"gain_rows{b}") for b in range(HB)]
         weights = keep.tile([P, S], F32, name="weights")
         cache = [keep.tile([P, T2], F32, name=f"cache{n}") for n in range(NT)]
         one = keep.tile([P, 1], F32, name="one")
@@ -70,18 +71,18 @@ def tile_list_posting_term_expansion_kernel(
         raw = {}
 
         def load_w1(b, a, parts=1):
-            raw[b, a] = stage.tile([P, PACK, PASS], F32, name="raw", bufs=3)
+            raw[b, a] = stage.tile([P, PACK, PASS], F32, name="raw", bufs=4)
             block = w1[PASS * a : PASS * (a + 1), PASS * b : PASS * (b + 1)].rearrange("(p j) c -> p j c", j=PACK)
             for c0 in range(0, PASS, PASS // parts):
                 cols = slice(c0, c0 + PASS // parts)
                 nc.sync.dma_start(raw[b, a][:, :, cols], block[:, :, cols])
 
-        load_w1(1, 0)
         load_w1(0, 0)
         load_table(1)
         load_w1(0, 1)
         load_table(2)
         load_w1(0, 2)
+        load_w1(1, 0)
         load_w1(1, 1)
         load_w1(1, 2, parts=2)
         nc.sync.dma_start(w4_w[:], w4_words.rearrange("b p c -> p b c").bitcast(I32))
@@ -90,13 +91,16 @@ def tile_list_posting_term_expansion_kernel(
                 w4_s[32 * q : 32 * q + 4, :, :],
                 w4_scales[:, 4 * q : 4 * q + 4, :].rearrange("b r n -> r b n").bitcast(I32),
             )
-        nc.sync.dma_start(weights[:], wgo)
         nc.sync.dma_start(places[:], offs2)
+        nc.sync.dma_start(weights[:], wgo)
 
-        nc.vector.tensor_copy(v_w[0][:], tab_w[0][:].bitcast(U32).indirect(picks[:]))
-        nc.vector.tensor_copy(v_s[:], tab_s[:].bitcast(U8).indirect(picks[:]))
-        for a in range(1, KA):
-            nc.vector.tensor_copy(v_w[a][:], tab_w[a][:].bitcast(U32).indirect(picks[:]))
+        for b in range(HB):
+            nc.scalar.copy(gain_rows[b][:], gains[:, b, :].unsqueeze(1).to_broadcast([P, P, PACK]))
+
+        def gather(dst, window, parts=1):
+            for c0 in range(0, S, S // parts):
+                c1 = c0 + S // parts
+                nc.vector.tensor_copy(dst[:, c0:c1], window.indirect(picks[:, c0 // LIST : c1 // LIST]))
 
         w1_w, w1_s = {}, {}
 
@@ -121,72 +125,76 @@ def tile_list_posting_term_expansion_kernel(
         def bank(i):
             return psum.tile([P, BANK], F32, name=f"bank{i}")
 
-        def runs(width):
-            return [(0, 256)] if width == 256 else [(0, 256), (256, 384)]
+        def first_passes(x_sum, b, a, u):
+            cols = slice(P * u, P * (u + 1))
+            for t in range(PACK):
+                rows = slice(P * t, P * (t + 1))
+                nc.tensor.matmul_mx(
+                    x_sum[:, rows],
+                    lhsT=w1_w[b, a][:, rows].bitcast(FP8X4),
+                    lhsT_scale=w1_s[b, a][:, rows],
+                    rhs=v_w[a][:, cols].bitcast(FP8X4),
+                    rhs_scale=v_s[4 * a : P, cols],
+                    start=(a == 0 and t == 0),
+                    stop=(a == KA - 1 and t == PACK - 1),
+                )
 
-        def first_pass(x_sum, b, a, t, c0, c1, start):
-            rows = slice(P * t, P * (t + 1))
-            cols = slice(start + c0, start + c1)
-            nc.tensor.matmul_mx(
-                x_sum[:, c0:c1],
-                lhsT=w1_w[b, a][:, rows].bitcast(FP8X4),
-                lhsT_scale=w1_s[b, a][:, rows],
-                rhs=v_w[a][:, cols].bitcast(FP8X4),
-                rhs_scale=v_s[4 * a : P, cols],
-                start=(a == 0),
-                stop=(a == KA - 1),
-            )
-
-        def first_product(b, piece, t, bank_index):
-            start, width = PIECES[piece]
+        def first_product(b, u, bank_index):
             x_sum = bank(bank_index)
-            for c0, c1 in runs(width):
-                for a in range(KA):
-                    first_pass(x_sum, b, a, t, c0, c1, start)
+            for a in range(KA):
+                first_passes(x_sum, b, a, u)
             return x_sum
 
-        def saturate(sum_of, piece, vector_planes=()):
-            width = PIECES[piece][1]
-            x = stage.tile([P, PACK, width], F32, name="x", bufs=4)
-            for t in range(PACK):
-                if t in vector_planes:
-                    nc.vector.tensor_scalar_max(x[:, t, :], sum_of(t)[:, :width], 0.0)
-                else:
-                    nc.scalar.activation(x[:, t, :], sum_of(t)[:, :width], ACT.Relu)
-                if t > 0:
-                    nc.scalar.activation(x[:, t - 1, :], x[:, t - 1, :], ACT.Ln, bias=1.0)
-            nc.scalar.activation(x[:, PACK - 1, :], x[:, PACK - 1, :], ACT.Ln, bias=1.0)
+        h_w = [keep.tile([P, S], U32, name=f"h_w{b}", align_bytes=64) for b in range(HB)]
+        h_s = [keep.tile([P, S], U8, name=f"h_s{b}", align_bytes=64) for b in range(HB)]
+
+        def woven_relu(x_sum, name, engine="scalar"):
+            x = keep.tile([P, P, PACK], F32, name=name)[:]
+            woven = x_sum[:].rearrange("p (t c) -> p c t", t=PACK)
+            if engine == "scalar":
+                nc.scalar.activation(x, woven, ACT.Relu)
+            else:
+                nc.vector.tensor_scalar_max(x, woven, 0.0)
             return x
 
-        def features(b, piece, banks):
-            return saturate(lambda t: first_product(b, piece, t, banks[t]), piece)
+        def woven_log(x):
+            nc.scalar.activation(x, x, ACT.Ln, bias=1.0)
+            return x
 
-        h_w, h_s = {}, {}
+        def woven_gain(x, b):
+            feat = stage.tile([P, P * PACK], BF16, name="feat", bufs=3, align_bytes=64)
+            nc.vector.tensor_tensor(feat[:].rearrange("p (c t) -> p c t", t=PACK), x, gain_rows[b][:], ALU.mult)
+            return feat
 
-        def quantise_h(x, b, piece, engine, slot):
-            width = PIECES[piece][1]
-            feat = keep.tile([P, PACK * width], BF16, name=f"feat{slot}", align_bytes=64)
-            h_w[b, piece] = keep.tile([P, width], U32, name=f"h_w{b}{piece}", align_bytes=64)
-            h_s[b, piece] = keep.tile([P, width], U8, name=f"h_s{b}{piece}", align_bytes=64)
-            if engine == "scalar":
-                planes = keep.tile([P, PACK, width], BF16, name=f"planes{b}{piece}")
-                for t in range(PACK):
-                    nc.scalar.activation(planes[:, t, :], x[:, t, :], ACT.Copy, scale=gains[:, b, t : t + 1])
-            for c0, c1 in runs(width):
-                dst = feat[:, PACK * c0 : PACK * c1].rearrange("p (c t) -> p c t", t=PACK)
-                if engine == "scalar":
-                    nc.scalar.copy(dst, planes[:, :, c0:c1].rearrange("p t c -> p c t"))
-                else:
-                    nc.vector.tensor_tensor(
-                        dst,
-                        x[:, :, c0:c1].rearrange("p t c -> p c t"),
-                        gains[:, b, :].unsqueeze(1).to_broadcast([P, c1 - c0, PACK]),
-                        ALU.mult,
-                    )
-            for c0, c1 in runs(width):
-                nc.vector.quantize_mx(
-                    h_w[b, piece][:, c0:c1].bitcast(FP8X4), h_s[b, piece][:, c0:c1], feat[:, PACK * c0 : PACK * c1]
+        def quantise_h(feat, b, c0, c1):
+            nc.vector.quantize_mx(h_w[b][:, c0:c1].bitcast(FP8X4), h_s[b][:, c0:c1], feat)
+
+        def plane_features(b, piece, banks):
+            start, width = PIECES[piece]
+            if b == 0:
+                x = keep.tile([P, PACK, width], F32, name="x_planes")
+            else:
+                x = stage.tile([P, PACK, width], F32, name="raw", bufs=4)
+            for i in range(width // P):
+                x_sum = first_product(b, start // P + i, banks[i]) if isinstance(banks[i], int) else banks[i]
+                part = x[:, :, P * i : P * (i + 1)]
+                nc.scalar.activation(part, x_sum[:].rearrange("p (t c) -> p t c", t=PACK), ACT.Relu)
+                nc.scalar.activation(part, part, ACT.Ln, bias=1.0)
+            return x
+
+        def plane_gain(x, b, piece):
+            start, width = PIECES[piece]
+            planes = keep.tile([P, PACK, width], BF16, name=f"planes{b}{piece}")
+            feat = keep.tile([P, PACK * width], BF16, name=f"woven{b}", align_bytes=64)
+            for t in range(PACK):
+                nc.scalar.activation(planes[:, t, :], x[:, t, :], ACT.Copy, scale=gains[:, b, t : t + 1])
+            for c0, c1 in [(0, 256), (256, width)]:
+                nc.scalar.copy(
+                    feat[:, PACK * c0 : PACK * c1].rearrange("p (c i t) -> p c t i", i=4, t=PACK),
+                    planes[:, :, c0:c1].rearrange("p t (c i) -> p c t i", i=4),
                 )
+            for c0, c1 in [(0, 256), (256, width)]:
+                quantise_h(feat[:, PACK * c0 : PACK * c1], b, start + c0, start + c1)
 
         w4_bytes = w4_w[:].bitcast(U8)
         w4_scale_bytes = w4_s[:].bitcast(U8)
@@ -204,13 +212,13 @@ def tile_list_posting_term_expansion_kernel(
                             y_sum[:, c0 : c0 + P],
                             lhsT=w4_bytes[:, b, 2 * P * n : 2 * P * (n + 1)].bitcast(FP4X4),
                             lhsT_scale=w4_scale_bytes[:, b, P * n : P * (n + 1)],
-                            rhs=h_w[b, piece][:, c0 : c0 + P].bitcast(FP8X4),
-                            rhs_scale=h_s[b, piece][:, c0 : c0 + P],
+                            rhs=h_w[b][:, start + c0 : start + c0 + P].bitcast(FP8X4),
+                            rhs_scale=h_s[b][:, start + c0 : start + c0 + P],
                             start=(b == 0),
                             stop=(b == HB - 1),
                         )
                 if held is None:
-                    y = stage.tile([P, width], F32, name="y", bufs=8)[:]
+                    y = stage.tile([P, width], F32, name="y", bufs=7)[:]
                 else:
                     y = late[:, n - tiles[0], :]
                 nc.scalar.activation(y, y_sum[:, :width], ACT.Relu)
@@ -220,32 +228,37 @@ def tile_list_posting_term_expansion_kernel(
                 if piece == len(PIECES) - 1:
                     nc.sync.dma_start(out[P * n : P * (n + 1), :], cache[n][:])
 
-        first_width = PIECES[0][1]
-
-        quantise_w1(1, 0, [("scalar", 0, P)], PASS)
-        sums = [bank(t) for t in range(PACK)]
+        gather(v_w[0], tab_w[0][:].bitcast(U32))
+        gather(v_s, tab_s[:].bitcast(U8))
+        early = [bank(u) for u in range(4)]
         for a in range(KA):
+            if a > 0:
+                gather(v_w[a], tab_w[a][:].bitcast(U32), parts=2 if a == KA - 1 else 1)
             quantise_w1(0, a, [("scalar", 0, P)] if a < KA - 1 else [("scalar", 0, 44), ("vector", 44, P)], PASS)
-            for t in range(PACK):
-                first_pass(sums[t], 0, a, t, 0, first_width, 0)
-        x00 = saturate(lambda t: sums[t], 0)
+            for u in range(4):
+                first_passes(early[u], 0, a, u)
 
-        quantise_w1(1, 1, [("vector", 0, P)], PASS)
-        quantise_w1(1, 2, [("vector", 0, 64), ("vector", 64, 106), ("scalar", 106, P)], P)
-        sums = [bank(PACK + t) for t in range(PACK)]
-        for a in range(KA):
-            for t in range(PACK):
-                first_pass(sums[t], 1, a, t, 0, first_width, 0)
-        x10 = saturate(lambda t: sums[t], 0, (1, 3))
-        x01 = features(0, 1, [0, 1, 2, 3])
-        quantise_h(x10, 1, 0, "vector", 0)
-        quantise_h(x00, 0, 0, "vector", 1)
-        quantise_h(x01, 0, 1, "vector", 0)
-        expansion(0, [0, 1, 2, 3])
-        quantise_h(features(1, 1, [4, 5, 4, 5]), 1, 1, "scalar", 1)
-        expansion(0, [4, 5], "planes11")
+        for u in range(2):
+            x0 = woven_log(woven_relu(early[u], f"x0{u}"))
+            quantise_h(woven_gain(x0, 0)[:], 0, P * u, P * (u + 1))
+
+        lead = [bank(4 + u) for u in range(2)]
+        for a in range(KA - 1):
+            quantise_w1(1, a, [("vector", 0, P)], PASS)
+            for u in range(2):
+                first_passes(lead[u], 1, a, u)
+        quantise_w1(1, KA - 1, [("vector", 0, 64), ("vector", 64, 106), ("scalar", 106, P)], P)
+        for u in range(2):
+            first_passes(lead[u], 1, KA - 1, u)
+        x1 = [woven_relu(lead[0], "x10"), woven_relu(lead[1], "planes01", "vector")]
+        for u in range(2):
+            quantise_h(woven_gain(woven_log(x1[u]), 1)[:], 1, P * u, P * (u + 1))
+        expansion(0, [0, 1, 2, 3, 4])
+        plane_gain(plane_features(0, 1, [early[2], early[3], 0]), 0, 1)
+        plane_gain(plane_features(1, 1, [4, 5, 1]), 1, 1)
+        expansion(0, [5], "planes11")
         expansion(1, [0, 1, 2, 3, 4])
-        quantise_h(features(0, 2, [0, 1, 2, 3]), 0, 2, "scalar", 0)
-        quantise_h(features(1, 2, [0, 1, 2, 3]), 1, 2, "scalar", 1)
+        plane_gain(plane_features(0, 2, [2, 3, 0]), 0, 2)
+        plane_gain(plane_features(1, 2, [4, 5, 1]), 1, 2)
         expansion(1, [5], "planes12")
         expansion(2, range(NT))

@@ -161,20 +161,34 @@ def tile_list_posting_term_expansion_kernel(
             nc.scalar.activation(x, x, ACT.Ln, bias=1.0)
             return x
 
-        def woven_gain(x, b):
-            feat = stage.tile([P, P * PACK], BF16, name="feat", bufs=3, align_bytes=64)
+        def woven_gain(x, b, name):
+            feat = keep.tile([P, P * PACK], BF16, name=name, align_bytes=64)
             nc.vector.tensor_tensor(feat[:].rearrange("p (c t) -> p c t", t=PACK), x, gain_rows[b][:], ALU.mult)
             return feat
 
         def quantise_h(feat, b, c0, c1):
             nc.vector.quantize_mx(h_w[b][:, c0:c1].bitcast(FP8X4), h_s[b][:, c0:c1], feat)
 
+        def woven_piece(b, piece, banks, held):
+            start, width = PIECES[piece]
+            x = keep.tile([P, width // P, P, PACK], F32, name=f"x_woven{piece}")
+            for i in range(width // P):
+                x_sum = first_product(b, start // P + i, banks[i]) if isinstance(banks[i], int) else banks[i]
+                nc.scalar.activation(x[:, i], x_sum[:].rearrange("p (t c) -> p c t", t=PACK), ACT.Relu)
+                nc.scalar.activation(x[:, i], x[:, i], ACT.Ln, bias=1.0)
+            feat = keep.tile([P, PACK * width], BF16, name=held, align_bytes=64)
+            nc.vector.tensor_tensor(
+                feat[:].rearrange("p (i e) -> p i e", e=P * PACK),
+                x[:].rearrange("p i c t -> p i (c t)"),
+                gain_rows[b][:].rearrange("p c t -> p (c t)").unsqueeze(1).to_broadcast([P, width // P, P * PACK]),
+                ALU.mult,
+            )
+            for c0, c1 in [(0, 256), (256, width)]:
+                quantise_h(feat[:, PACK * c0 : PACK * c1], b, start + c0, start + c1)
+
         def plane_features(b, piece, banks):
             start, width = PIECES[piece]
-            if b == 0:
-                x = keep.tile([P, PACK, width], F32, name="x_planes")
-            else:
-                x = stage.tile([P, PACK, width], F32, name="raw", bufs=4)
+            x = stage.tile([P, PACK, width], F32, name="raw", bufs=4)
             for i in range(width // P):
                 x_sum = first_product(b, start // P + i, banks[i]) if isinstance(banks[i], int) else banks[i]
                 part = x[:, :, P * i : P * (i + 1)]
@@ -190,8 +204,8 @@ def tile_list_posting_term_expansion_kernel(
                 nc.scalar.activation(planes[:, t, :], x[:, t, :], ACT.Copy, scale=gains[:, b, t : t + 1])
             for c0, c1 in [(0, 256), (256, width)]:
                 nc.scalar.copy(
-                    feat[:, PACK * c0 : PACK * c1].rearrange("p (c i t) -> p c t i", i=4, t=PACK),
-                    planes[:, :, c0:c1].rearrange("p t (c i) -> p c t i", i=4),
+                    feat[:, PACK * c0 : PACK * c1].rearrange("p (c t) -> p c t", t=PACK),
+                    planes[:, :, c0:c1].rearrange("p t c -> p c t"),
                 )
             for c0, c1 in [(0, 256), (256, width)]:
                 quantise_h(feat[:, PACK * c0 : PACK * c1], b, start + c0, start + c1)
@@ -240,7 +254,7 @@ def tile_list_posting_term_expansion_kernel(
 
         for u in range(2):
             x0 = woven_log(woven_relu(early[u], f"x0{u}"))
-            quantise_h(woven_gain(x0, 0)[:], 0, P * u, P * (u + 1))
+            quantise_h(woven_gain(x0, 0, f"feat0{u}")[:], 0, P * u, P * (u + 1))
 
         lead = [bank(4 + u) for u in range(2)]
         for a in range(KA - 1):
@@ -250,15 +264,15 @@ def tile_list_posting_term_expansion_kernel(
         quantise_w1(1, KA - 1, [("vector", 0, 64), ("vector", 64, 106), ("scalar", 106, P)], P)
         for u in range(2):
             first_passes(lead[u], 1, KA - 1, u)
-        x1 = [woven_relu(lead[0], "x10"), woven_relu(lead[1], "planes01", "vector")]
+        x1 = [woven_relu(lead[0], "x10"), woven_relu(lead[1], "x_woven2", "vector")]
         for u in range(2):
-            quantise_h(woven_gain(woven_log(x1[u]), 1)[:], 1, P * u, P * (u + 1))
+            quantise_h(woven_gain(woven_log(x1[u]), 1, f"feat1{u}")[:], 1, P * u, P * (u + 1))
         expansion(0, [0, 1, 2, 3, 4])
-        plane_gain(plane_features(0, 1, [early[2], early[3], 0]), 0, 1)
+        woven_piece(0, 1, [early[2], early[3], 0], "feat11")
         plane_gain(plane_features(1, 1, [4, 5, 1]), 1, 1)
         expansion(0, [5], "planes11")
         expansion(1, [0, 1, 2, 3, 4])
-        plane_gain(plane_features(0, 2, [2, 3, 0]), 0, 2)
+        woven_piece(0, 2, [2, 3, 0], "feat11")
         plane_gain(plane_features(1, 2, [4, 5, 1]), 1, 2)
         expansion(1, [5], "planes12")
         expansion(2, range(NT))

@@ -50,31 +50,40 @@ def tile_list_posting_term_expansion_kernel(
         one = keep.tile([P, 1], F32, name="one")
         warm = keep.tile([P, 1], F32, name="warm")
 
-        nc.vector.memset(tab_s[:], 0)
+        nc.gpsimd.memset(tab_s[:], 0)
+        for q in range(4):
+            nc.gpsimd.dma_start(
+                tab_s[32 * q : 32 * q + 4 * KA, :], tab_scales[:, 4 * q : 4 * q + 4, :].bitcast(I32)
+            )
+        nc.vector.memset(w4_s[:], 0)
         nc.vector.memset(one[:], 1.0)
         nc.scalar.activation(warm[:], one[:], ACT.Ln)
-        nc.vector.memset(w4_s[:], 0)
+        nc.gpsimd.dma_start(gains[:], gain.rearrange("(b p t) -> p b t", b=HB, t=PACK))
         for n in range(NT):
-            (nc.vector if n < 3 else nc.gpsimd).memset(cache[n][:], 0.0)
+            if n < 4:
+                nc.vector.memset(cache[n][:, : T2 // 2 - 1], 0.0)
+                nc.vector.memset(cache[n][:, T2 // 2 - 1 :], 0.0)
+            else:
+                nc.gpsimd.memset(cache[n][:], 0.0)
+        for q in range(4):
+            nc.gpsimd.dma_start(
+                w4_s[32 * q : 32 * q + 4, :, :],
+                w4_scales[:, 4 * q : 4 * q + 4, :].rearrange("b r n -> r b n").bitcast(I32),
+            )
 
         def load_table(a):
             nc.sync.dma_start(tab_w[a][:], tab_words[a].rearrange("p t i -> p (t i)").bitcast(I32))
 
         load_table(0)
         nc.sync.dma_start(picks[:], offs)
-        for q in range(4):
-            nc.sync.dma_start(
-                tab_s[32 * q : 32 * q + 4 * KA, :], tab_scales[:, 4 * q : 4 * q + 4, :].bitcast(I32)
-            )
-        nc.sync.dma_start(gains[:], gain.rearrange("(b p t) -> p b t", b=HB, t=PACK))
 
         raw = {}
 
-        def load_w1(b, a, parts=1):
-            raw[b, a] = stage.tile([P, PACK, PASS], F32, name="raw", bufs=4)
+        def load_w1(b, a, cuts=(0, PASS)):
+            raw[b, a] = keep.tile([P, PACK, PASS], F32, name=f"raw{(KA * b + a) % 4}")
             block = w1[PASS * a : PASS * (a + 1), PASS * b : PASS * (b + 1)].rearrange("(p j) c -> p j c", j=PACK)
-            for c0 in range(0, PASS, PASS // parts):
-                cols = slice(c0, c0 + PASS // parts)
+            for c0, c1 in zip(cuts, cuts[1:]):
+                cols = slice(c0, c1)
                 nc.sync.dma_start(raw[b, a][:, :, cols], block[:, :, cols])
 
         load_w1(0, 0)
@@ -84,13 +93,8 @@ def tile_list_posting_term_expansion_kernel(
         load_w1(0, 2)
         load_w1(1, 0)
         load_w1(1, 1)
-        load_w1(1, 2, parts=2)
+        load_w1(1, 2, (0, 384, PASS))
         nc.sync.dma_start(w4_w[:], w4_words.rearrange("b p c -> p b c").bitcast(I32))
-        for q in range(4):
-            nc.sync.dma_start(
-                w4_s[32 * q : 32 * q + 4, :, :],
-                w4_scales[:, 4 * q : 4 * q + 4, :].rearrange("b r n -> r b n").bitcast(I32),
-            )
         nc.sync.dma_start(places[:], offs2)
         nc.sync.dma_start(weights[:], wgo)
 
@@ -105,7 +109,10 @@ def tile_list_posting_term_expansion_kernel(
         w1_w, w1_s = {}, {}
 
         def quantise_w1(b, a, shares, quantise_width):
-            grouped = stage.tile([P, PACK * PASS], BF16, name="grouped", align_bytes=64)
+            if (b, a) == (HB - 1, KA - 1):
+                grouped = keep.tile([P, PACK * PASS], BF16, name="last_grouped", align_bytes=64)
+            else:
+                grouped = stage.tile([P, PACK * PASS], BF16, name="grouped", align_bytes=64)
             dst = grouped[:].rearrange("p (t m j) -> p m t j", t=PACK, j=PACK)
             src = raw[b, a][:].rearrange("p j (m t) -> p m t j", t=PACK)
             for engine, m0, m1 in shares:
@@ -148,13 +155,9 @@ def tile_list_posting_term_expansion_kernel(
         h_w = [keep.tile([P, S], U32, name=f"h_w{b}", align_bytes=64) for b in range(HB)]
         h_s = [keep.tile([P, S], U8, name=f"h_s{b}", align_bytes=64) for b in range(HB)]
 
-        def woven_relu(x_sum, name, engine="scalar"):
+        def woven_relu(x_sum, name):
             x = keep.tile([P, P, PACK], F32, name=name)[:]
-            woven = x_sum[:].rearrange("p (t c) -> p c t", t=PACK)
-            if engine == "scalar":
-                nc.scalar.activation(x, woven, ACT.Relu)
-            else:
-                nc.vector.tensor_scalar_max(x, woven, 0.0)
+            nc.scalar.activation(x, x_sum[:].rearrange("p (t c) -> p c t", t=PACK), ACT.Relu)
             return x
 
         def woven_log(x):
@@ -169,26 +172,20 @@ def tile_list_posting_term_expansion_kernel(
         def quantise_h(feat, b, c0, c1):
             nc.vector.quantize_mx(h_w[b][:, c0:c1].bitcast(FP8X4), h_s[b][:, c0:c1], feat)
 
-        def woven_piece(b, piece, banks, held):
+        def woven_piece(b, piece, banks, held, homes):
             start, width = PIECES[piece]
-            x = keep.tile([P, width // P, P, PACK], F32, name=f"x_woven{piece}")
+            x = [keep.tile([P, P, PACK], F32, name=home) for home in homes]
             for i in range(width // P):
                 x_sum = first_product(b, start // P + i, banks[i]) if isinstance(banks[i], int) else banks[i]
-                nc.scalar.activation(x[:, i], x_sum[:].rearrange("p (t c) -> p c t", t=PACK), ACT.Relu)
-                nc.scalar.activation(x[:, i], x[:, i], ACT.Ln, bias=1.0)
-            feat = keep.tile([P, PACK * width], BF16, name=held, align_bytes=64)
-            nc.vector.tensor_tensor(
-                feat[:].rearrange("p (i e) -> p i e", e=P * PACK),
-                x[:].rearrange("p i c t -> p i (c t)"),
-                gain_rows[b][:].rearrange("p c t -> p (c t)").unsqueeze(1).to_broadcast([P, width // P, P * PACK]),
-                ALU.mult,
-            )
-            for c0, c1 in [(0, 256), (256, width)]:
-                quantise_h(feat[:, PACK * c0 : PACK * c1], b, start + c0, start + c1)
+                nc.scalar.activation(x[i][:], x_sum[:].rearrange("p (t c) -> p c t", t=PACK), ACT.Relu)
+                nc.scalar.activation(x[i][:], x[i][:], ACT.Ln, bias=1.0)
+            feats = [woven_gain(x[i][:], b, name) for i, name in enumerate(held)]
+            for i, feat in enumerate(feats):
+                quantise_h(feat[:], b, start + P * i, start + P * (i + 1))
 
         def plane_features(b, piece, banks):
             start, width = PIECES[piece]
-            x = stage.tile([P, PACK, width], F32, name="raw", bufs=4)
+            x = keep.tile([P, PACK, width], F32, name={(1, 1): "x11", (0, 2): "raw3", (1, 2): "raw2"}[b, piece])
             for i in range(width // P):
                 x_sum = first_product(b, start // P + i, banks[i]) if isinstance(banks[i], int) else banks[i]
                 part = x[:, :, P * i : P * (i + 1)]
@@ -199,7 +196,7 @@ def tile_list_posting_term_expansion_kernel(
         def plane_gain(x, b, piece):
             start, width = PIECES[piece]
             planes = keep.tile([P, PACK, width], BF16, name=f"planes{b}{piece}")
-            feat = keep.tile([P, PACK * width], BF16, name=f"woven{b}", align_bytes=64)
+            feat = keep.tile([P, PACK * width], BF16, name="woven1" if b == 1 else "last_grouped", align_bytes=64)
             for t in range(PACK):
                 nc.scalar.activation(planes[:, t, :], x[:, t, :], ACT.Copy, scale=gains[:, b, t : t + 1])
             for c0, c1 in [(0, 256), (256, width)]:
@@ -231,8 +228,10 @@ def tile_list_posting_term_expansion_kernel(
                             start=(b == 0),
                             stop=(b == HB - 1),
                         )
-                if held is None:
-                    y = stage.tile([P, width], F32, name="y", bufs=7)[:]
+                if piece == 0 and n < 2:
+                    y = keep.tile([P, width], F32, name=["first_y", "second_y"][n], align_bytes=64)[:]
+                elif held is None:
+                    y = stage.tile([P, width], F32, name="y", bufs=5)[:]
                 else:
                     y = late[:, n - tiles[0], :]
                 nc.scalar.activation(y, y_sum[:, :width], ACT.Relu)
@@ -252,27 +251,29 @@ def tile_list_posting_term_expansion_kernel(
             for u in range(4):
                 first_passes(early[u], 0, a, u)
 
-        for u in range(2):
-            x0 = woven_log(woven_relu(early[u], f"x0{u}"))
-            quantise_h(woven_gain(x0, 0, f"feat0{u}")[:], 0, P * u, P * (u + 1))
-
         lead = [bank(4 + u) for u in range(2)]
         for a in range(KA - 1):
             quantise_w1(1, a, [("vector", 0, P)], PASS)
             for u in range(2):
                 first_passes(lead[u], 1, a, u)
-        quantise_w1(1, KA - 1, [("vector", 0, 64), ("vector", 64, 106), ("scalar", 106, P)], P)
+        x0 = [woven_log(woven_relu(early[u], f"x0{u}")) for u in range(2)]
+        quantise_w1(1, KA - 1, [("vector", 0, 96), ("vector", 96, P)], P)
         for u in range(2):
             first_passes(lead[u], 1, KA - 1, u)
-        x1 = [woven_relu(lead[0], "x10"), woven_relu(lead[1], "x_woven2", "vector")]
+        x1 = [woven_relu(lead[u], f"x1{u}") for u in range(2)]
+        x1 = [woven_log(x) for x in x1]
+        feat = keep.tile([P, 2, P, PACK], BF16, name="last_grouped", align_bytes=64)
         for u in range(2):
-            quantise_h(woven_gain(woven_log(x1[u]), 1, f"feat1{u}")[:], 1, P * u, P * (u + 1))
+            nc.vector.tensor_tensor(feat[:, u], x0[u], gain_rows[0][:], ALU.mult)
+        quantise_h(feat[:].rearrange("p u c t -> p (u c t)"), 0, 0, 2 * P)
+        for u in range(2):
+            quantise_h(woven_gain(x1[u], 1, f"feat1{u}")[:], 1, P * u, P * (u + 1))
         expansion(0, [0, 1, 2, 3, 4])
-        woven_piece(0, 1, [early[2], early[3], 0], "feat11")
-        plane_gain(plane_features(1, 1, [4, 5, 1]), 1, 1)
+        woven_piece(0, 1, [early[2], early[3], 0], ["feat11", "first_y", "second_y"], ["raw3", "raw0", "x10"])
+        plane_gain(plane_features(1, 1, [1, 4, 5]), 1, 1)
         expansion(0, [5], "planes11")
         expansion(1, [0, 1, 2, 3, 4])
-        woven_piece(0, 2, [2, 3, 0], "feat11")
+        plane_gain(plane_features(0, 2, [2, 3, 0]), 0, 2)
         plane_gain(plane_features(1, 2, [4, 5, 1]), 1, 2)
         expansion(1, [5], "planes12")
         expansion(2, range(NT))

@@ -22,7 +22,8 @@ KA = K // PASS
 HB = H // PASS
 NT = N // P
 BANK = 512
-PIECES = [(0, 256), (256, 384), (640, 384)]
+WIDTH = 256
+GATHER_PARTS = (1, 1, 2)
 LIST = 16
 
 
@@ -39,7 +40,10 @@ def tile_list_posting_term_expansion_kernel(
         places = keep.tile([P, S // LIST], U16, name="places")
         tab_w = [keep.tile([P, T], I32, name=f"tab_w{a}", align_bytes=64) for a in range(KA)]
         tab_s = keep.tile([P, T // 4], I32, name="tab_s", align_bytes=64)
-        v_w = [keep.tile([P, S], U32, name=f"v_w{a}", align_bytes=64) for a in range(KA)]
+        v_w = [
+            [keep.tile([P, S // parts], U32, name=f"v_w{a}{i}", align_bytes=64) for i in range(parts)]
+            for a, parts in enumerate(GATHER_PARTS)
+        ]
         v_s = keep.tile([P, S], U8, name="v_s", align_bytes=64)
         w4_w = keep.tile([P, HB, 2 * N // 4], I32, name="w4_w", align_bytes=64)
         w4_s = keep.tile([P, HB, N // 4], I32, name="w4_s", align_bytes=64)
@@ -53,7 +57,7 @@ def tile_list_posting_term_expansion_kernel(
         nc.gpsimd.memset(tab_s[:], 0)
         for q in range(4):
             nc.gpsimd.dma_start(
-                tab_s[32 * q : 32 * q + 4 * KA, :], tab_scales[:, 4 * q : 4 * q + 4, :].bitcast(I32)
+                tab_s[32 * q + 4 : 32 * q + 4 + 4 * KA, :], tab_scales[:, 4 * q : 4 * q + 4, :].bitcast(I32)
             )
         nc.vector.memset(w4_s[:], 0)
         nc.vector.memset(one[:], 1.0)
@@ -89,11 +93,11 @@ def tile_list_posting_term_expansion_kernel(
         load_w1(0, 0)
         load_table(1)
         load_w1(0, 1)
-        load_table(2)
         load_w1(0, 2)
+        load_table(2)
         load_w1(1, 0)
         load_w1(1, 1)
-        load_w1(1, 2, (0, 384, PASS))
+        load_w1(1, 2)
         nc.sync.dma_start(w4_w[:], w4_words.rearrange("b p c -> p b c").bitcast(I32))
         nc.sync.dma_start(places[:], offs2)
         nc.sync.dma_start(weights[:], wgo)
@@ -101,10 +105,10 @@ def tile_list_posting_term_expansion_kernel(
         for b in range(HB):
             nc.scalar.copy(gain_rows[b][:], gains[:, b, :].unsqueeze(1).to_broadcast([P, P, PACK]))
 
-        def gather(dst, window, parts=1):
-            for c0 in range(0, S, S // parts):
-                c1 = c0 + S // parts
-                nc.vector.tensor_copy(dst[:, c0:c1], window.indirect(picks[:, c0 // LIST : c1 // LIST]))
+        def gather(parts, window):
+            count = S // len(parts) // LIST
+            for i, part in enumerate(parts):
+                nc.vector.tensor_copy(part[:], window.indirect(picks[:, count * i : count * (i + 1)]))
 
         w1_w, w1_s = {}, {}
 
@@ -132,16 +136,17 @@ def tile_list_posting_term_expansion_kernel(
         def bank(i):
             return psum.tile([P, BANK], F32, name=f"bank{i}")
 
-        def first_passes(x_sum, b, a, u):
+        def first_passes(x_sum, b, a, u, slices=range(PACK)):
             cols = slice(P * u, P * (u + 1))
-            for t in range(PACK):
+            part, first = divmod(P * u, S // GATHER_PARTS[a])
+            for t in slices:
                 rows = slice(P * t, P * (t + 1))
                 nc.tensor.matmul_mx(
                     x_sum[:, rows],
                     lhsT=w1_w[b, a][:, rows].bitcast(FP8X4),
                     lhsT_scale=w1_s[b, a][:, rows],
-                    rhs=v_w[a][:, cols].bitcast(FP8X4),
-                    rhs_scale=v_s[4 * a : P, cols],
+                    rhs=v_w[a][part][:, first : first + P].bitcast(FP8X4),
+                    rhs_scale=v_s[4 * (a + 1) : P, cols],
                     start=(a == 0 and t == 0),
                     stop=(a == KA - 1 and t == PACK - 1),
                 )
@@ -172,83 +177,90 @@ def tile_list_posting_term_expansion_kernel(
         def quantise_h(feat, b, c0, c1):
             nc.vector.quantize_mx(h_w[b][:, c0:c1].bitcast(FP8X4), h_s[b][:, c0:c1], feat)
 
-        def woven_piece(b, piece, banks, held, homes):
-            start, width = PIECES[piece]
-            x = [keep.tile([P, P, PACK], F32, name=home) for home in homes]
-            for i in range(width // P):
-                x_sum = first_product(b, start // P + i, banks[i]) if isinstance(banks[i], int) else banks[i]
-                nc.scalar.activation(x[i][:], x_sum[:].rearrange("p (t c) -> p c t", t=PACK), ACT.Relu)
-                nc.scalar.activation(x[i][:], x[i][:], ACT.Ln, bias=1.0)
-            feats = [woven_gain(x[i][:], b, name) for i, name in enumerate(held)]
-            for i, feat in enumerate(feats):
-                quantise_h(feat[:], b, start + P * i, start + P * (i + 1))
-
-        def plane_features(b, piece, banks):
-            start, width = PIECES[piece]
-            x = keep.tile([P, PACK, width], F32, name={(1, 1): "x11", (0, 2): "raw3", (1, 2): "raw2"}[b, piece])
-            for i in range(width // P):
-                x_sum = first_product(b, start // P + i, banks[i]) if isinstance(banks[i], int) else banks[i]
-                part = x[:, :, P * i : P * (i + 1)]
-                nc.scalar.activation(part, x_sum[:].rearrange("p (t c) -> p t c", t=PACK), ACT.Relu)
-                nc.scalar.activation(part, part, ACT.Ln, bias=1.0)
+        def plane_relu(x_sum, name):
+            x = keep.tile([P, PACK * P], F32, name=name)
+            nc.scalar.activation(x[:], x_sum[:], ACT.Relu)
             return x
 
-        def plane_gain(x, b, piece):
-            start, width = PIECES[piece]
-            planes = keep.tile([P, PACK, width], BF16, name=f"planes{b}{piece}")
-            feat = keep.tile([P, PACK * width], BF16, name="woven1" if b == 1 else "last_grouped", align_bytes=64)
+        def plane_log(x):
+            nc.scalar.activation(x[:], x[:], ACT.Ln, bias=1.0)
+
+        def plane_gain(x, b, name):
+            planes = keep.tile([P, PACK, P], BF16, name=name)
             for t in range(PACK):
-                nc.scalar.activation(planes[:, t, :], x[:, t, :], ACT.Copy, scale=gains[:, b, t : t + 1])
-            for c0, c1 in [(0, 256), (256, width)]:
-                nc.scalar.copy(
-                    feat[:, PACK * c0 : PACK * c1].rearrange("p (c t) -> p c t", t=PACK),
-                    planes[:, :, c0:c1].rearrange("p t c -> p c t"),
-                )
-            for c0, c1 in [(0, 256), (256, width)]:
-                quantise_h(feat[:, PACK * c0 : PACK * c1], b, start + c0, start + c1)
+                nc.scalar.activation(planes[:, t, :], x[:, P * t : P * (t + 1)], ACT.Copy, scale=gains[:, b, t : t + 1])
+            return planes
+
+        def weave(feat, i, planes):
+            nc.scalar.copy(
+                feat[:, PASS * i : PASS * (i + 1)].rearrange("p (c e t) -> p c t e", e=PACK, t=PACK),
+                planes[:].rearrange("p t (c e) -> p c t e", e=PACK),
+            )
+
+        def finish_pair(xs, b, piece, home="planes"):
+            planes = [plane_gain(x, b, f"{home}{i}") for i, x in enumerate(xs)]
+            feat = keep.tile([P, 2 * PASS], BF16, name=f"feat{b}{piece}", align_bytes=64)
+            for i in range(2):
+                weave(feat, i, planes[i])
+            quantise_h(feat[:], b, WIDTH * piece, WIDTH * (piece + 1))
+            return feat
 
         w4_bytes = w4_w[:].bitcast(U8)
         w4_scale_bytes = w4_s[:].bitcast(U8)
 
-        def expansion(piece, tiles, held=None):
-            start, width = PIECES[piece]
-            entries = places[:, start // LIST : (start + width) // LIST]
-            if held is not None:
-                late = keep.tile([P, len(tiles), width], F32, name=held)
-            for n in tiles:
-                y_sum = bank(6 + n % 2)
-                for c0 in range(0, width, P):
-                    for b in range(HB):
-                        nc.tensor.matmul_mx(
-                            y_sum[:, c0 : c0 + P],
-                            lhsT=w4_bytes[:, b, 2 * P * n : 2 * P * (n + 1)].bitcast(FP4X4),
-                            lhsT_scale=w4_scale_bytes[:, b, P * n : P * (n + 1)],
-                            rhs=h_w[b][:, start + c0 : start + c0 + P].bitcast(FP8X4),
-                            rhs_scale=h_s[b][:, start + c0 : start + c0 + P],
-                            start=(b == 0),
-                            stop=(b == HB - 1),
-                        )
-                if piece == 0 and n < 2:
-                    y = keep.tile([P, width], F32, name=["first_y", "second_y"][n], align_bytes=64)[:]
-                elif held is None:
-                    y = stage.tile([P, width], F32, name="y", bufs=5)[:]
-                else:
-                    y = late[:, n - tiles[0], :]
-                nc.scalar.activation(y, y_sum[:, :width], ACT.Relu)
-                nc.vector.tensor_tensor(
-                    cache[n][:].indirect(entries), y, weights[:, start : start + width], ALU.mult
-                )
-                if piece == len(PIECES) - 1:
-                    nc.sync.dma_start(out[P * n : P * (n + 1), :], cache[n][:])
+        y_tiles = {}
+        y_count = []
+
+        def expansion(piece, n, pieces=1):
+            start, width = WIDTH * piece, WIDTH * pieces
+            if pieces > 1:
+                y = keep.tile([P, width], F32, name=f"x0{n - 4}")[:]
+            else:
+                if piece not in y_tiles:
+                    y_tiles[piece] = keep.tile([P, NT, WIDTH], F32, name=f"raw{(piece + 2) % 4}")
+                y = y_tiles[piece][:, n, :]
+            y_sum = bank(6 + len(y_count) % 2)
+            y_count.append(n)
+            for c0 in range(0, width, P):
+                for b in range(HB):
+                    nc.tensor.matmul_mx(
+                        y_sum[:, c0 : c0 + P],
+                        lhsT=w4_bytes[:, b, 2 * P * n : 2 * P * (n + 1)].bitcast(FP4X4),
+                        lhsT_scale=w4_scale_bytes[:, b, P * n : P * (n + 1)],
+                        rhs=h_w[b][:, start + c0 : start + c0 + P].bitcast(FP8X4),
+                        rhs_scale=h_s[b][:, start + c0 : start + c0 + P],
+                        start=(b == 0),
+                        stop=(b == HB - 1),
+                    )
+            nc.scalar.activation(y, y_sum[:, :width], ACT.Relu)
+            nc.vector.tensor_tensor(
+                cache[n][:].indirect(places[:, start // LIST : (start + width) // LIST]),
+                y,
+                weights[:, start : start + width],
+                ALU.mult,
+            )
+            if start + width == S:
+                nc.sync.dma_start(out[P * n : P * (n + 1), :], cache[n][:])
+
+        def plane_pair(b, piece, banks, between):
+            sums = [first_product(b, 2 * piece + i, banks[i]) for i in range(2)]
+            xs = [plane_relu(sums[i], f"xp{i}") for i in range(2)]
+            for step in between[:1]:
+                expansion(*step)
+            for x in xs:
+                plane_log(x)
+            for step in between[1:]:
+                expansion(*step)
+            return finish_pair(xs, b, piece)
 
         gather(v_w[0], tab_w[0][:].bitcast(U32))
-        gather(v_s, tab_s[:].bitcast(U8))
-        early = [bank(u) for u in range(4)]
+        gather([v_s], tab_s[:].bitcast(U8))
+        early = [bank(i) for i in (0, 1, 2, 3, 6, 7)]
         for a in range(KA):
+            quantise_w1(0, a, [("scalar", 0, P)], PASS)
             if a > 0:
-                gather(v_w[a], tab_w[a][:].bitcast(U32), parts=2 if a == KA - 1 else 1)
-            quantise_w1(0, a, [("scalar", 0, P)] if a < KA - 1 else [("scalar", 0, 44), ("vector", 44, P)], PASS)
-            for u in range(4):
+                gather(v_w[a], tab_w[a][:].bitcast(U32))
+            for u in range(6):
                 first_passes(early[u], 0, a, u)
 
         lead = [bank(4 + u) for u in range(2)]
@@ -257,23 +269,54 @@ def tile_list_posting_term_expansion_kernel(
             for u in range(2):
                 first_passes(lead[u], 1, a, u)
         x0 = [woven_log(woven_relu(early[u], f"x0{u}")) for u in range(2)]
-        quantise_w1(1, KA - 1, [("vector", 0, 96), ("vector", 96, P)], P)
+        quantise_w1(1, KA - 1, [("vector", 0, P)], 2 * P)
+        for slices in ((0, 1), (2, 3)):
+            for u in range(2):
+                first_passes(lead[u], 1, KA - 1, u, slices)
+        halves = [slice(c0, c0 + P // 2) for c0 in (0, P // 2)]
+        x1 = [keep.tile([P, P, PACK], F32, name=f"x1{u}") for u in range(2)]
         for u in range(2):
-            first_passes(lead[u], 1, KA - 1, u)
-        x1 = [woven_relu(lead[u], f"x1{u}") for u in range(2)]
-        x1 = [woven_log(x) for x in x1]
-        feat = keep.tile([P, 2, P, PACK], BF16, name="last_grouped", align_bytes=64)
-        for u in range(2):
+            for half in halves:
+                nc.scalar.activation(
+                    x1[u][:, half], lead[u][:].rearrange("p (t c) -> p c t", t=PACK)[:, half], ACT.Relu
+                )
+            for half in halves:
+                woven_log(x1[u][:, half])
+        x0.extend(woven_relu(early[u], f"x0{u}") for u in (2, 3))
+        for u in (2, 3):
+            woven_log(x0[u])
+        feat = keep.tile([P, 3, P, PACK], BF16, name="last_grouped", align_bytes=64)
+        for u in range(3):
             nc.vector.tensor_tensor(feat[:, u], x0[u], gain_rows[0][:], ALU.mult)
-        quantise_h(feat[:].rearrange("p u c t -> p (u c t)"), 0, 0, 2 * P)
-        for u in range(2):
-            quantise_h(woven_gain(x1[u], 1, f"feat1{u}")[:], 1, P * u, P * (u + 1))
-        expansion(0, [0, 1, 2, 3, 4])
-        woven_piece(0, 1, [early[2], early[3], 0], ["feat11", "first_y", "second_y"], ["raw3", "raw0", "x10"])
-        plane_gain(plane_features(1, 1, [1, 4, 5]), 1, 1)
-        expansion(0, [5], "planes11")
-        expansion(1, [0, 1, 2, 3, 4])
-        plane_gain(plane_features(0, 2, [2, 3, 0]), 0, 2)
-        plane_gain(plane_features(1, 2, [4, 5, 1]), 1, 2)
-        expansion(1, [5], "planes12")
-        expansion(2, range(NT))
+        first = woven_gain(x1[0][:], 1, "feat1w0")
+        quantise_h(feat[:, 0:2].rearrange("p u c t -> p (u c t)"), 0, 0, 2 * P)
+        quantise_h(first[:], 1, 0, P)
+        second = keep.tile([P, P, PACK], BF16, name="feat1w1", align_bytes=64)
+        for c0 in (0, P // 2):
+            half = slice(c0, c0 + P // 2)
+            nc.vector.tensor_tensor(second[:, half], x1[1][:, half], gain_rows[1][:, half], ALU.mult)
+        quantise_h(feat[:, 2].rearrange("p c t -> p (c t)"), 0, 2 * P, 3 * P)
+        quantise_h(second[:].rearrange("p c t -> p (c t)"), 1, P, 2 * P)
+        quantise_h(woven_gain(x0[3], 0, "feat1w1")[:], 0, 3 * P, 4 * P)
+        expansion(0, 0)
+        expansion(0, 1)
+        ahead = [plane_relu(early[4 + i], f"xa{i}") for i in range(2)]
+        for x in ahead:
+            plane_log(x)
+        plane_pair(1, 1, [0, 1], [(0, 2), (0, 3)])
+        expansion(0, 4)
+        expansion(0, 5)
+        finish_pair(ahead, 0, 2, "x1")
+        expansion(1, 0)
+        expansion(1, 1)
+        plane_pair(1, 2, [2, 3], [(1, 2), (1, 3)])
+        expansion(1, 4)
+        expansion(1, 5)
+        plane_pair(0, 3, [4, 5], [])
+        expansion(2, 0)
+        plane_pair(1, 3, [0, 1], [(2, 1), (2, 2)])
+        expansion(2, 3)
+        for n in range(4):
+            expansion(3, n)
+        for n in range(4, NT):
+            expansion(2, n, pieces=2)

@@ -51,8 +51,6 @@ def tile_list_posting_term_expansion_kernel(
         gain_rows = [keep.tile([P, P, PACK], F32, name=f"gain_rows{b}") for b in range(HB)]
         weights = keep.tile([P, S], F32, name="weights")
         cache = [keep.tile([P, T2], F32, name=f"cache{n}") for n in range(NT)]
-        one = keep.tile([P, 1], F32, name="one")
-        warm = keep.tile([P, 1], F32, name="warm")
 
         nc.gpsimd.memset(tab_s[:], 0)
         for q in range(4):
@@ -60,8 +58,6 @@ def tile_list_posting_term_expansion_kernel(
                 tab_s[32 * q + 4 : 32 * q + 4 + 4 * KA, :], tab_scales[:, 4 * q : 4 * q + 4, :].bitcast(I32)
             )
         nc.vector.memset(w4_s[:], 0)
-        nc.vector.memset(one[:], 1.0)
-        nc.scalar.activation(warm[:], one[:], ACT.Ln)
         nc.gpsimd.dma_start(gains[:], gain.rearrange("(b p t) -> p b t", b=HB, t=PACK))
         for n in range(NT):
             if n < 4:

@@ -58,6 +58,8 @@ def tile_list_posting_term_expansion_kernel(
                 tab_s[32 * q + 4 : 32 * q + 4 + 4 * KA, :], tab_scales[:, 4 * q : 4 * q + 4, :].bitcast(I32)
             )
         nc.vector.memset(w4_s[:], 0)
+        zeros = keep.tile([P, P], F32, name="zeros")
+        nc.vector.memset(zeros[:], 0.0)
         nc.gpsimd.dma_start(gains[:], gain.rearrange("(b p t) -> p b t", b=HB, t=PACK))
         for n in range(NT):
             if n < 4:
@@ -147,12 +149,6 @@ def tile_list_posting_term_expansion_kernel(
                     stop=(a == KA - 1 and t == PACK - 1),
                 )
 
-        def first_product(b, u, bank_index):
-            x_sum = bank(bank_index)
-            for a in range(KA):
-                first_passes(x_sum, b, a, u)
-            return x_sum
-
         h_w = [keep.tile([P, S], U32, name=f"h_w{b}", align_bytes=64) for b in range(HB)]
         h_s = [keep.tile([P, S], U8, name=f"h_s{b}", align_bytes=64) for b in range(HB)]
 
@@ -165,39 +161,52 @@ def tile_list_posting_term_expansion_kernel(
             nc.scalar.activation(x, x, ACT.Ln, bias=1.0)
             return x
 
-        def woven_gain(x, b, name):
-            feat = keep.tile([P, P * PACK], BF16, name=name, align_bytes=64)
-            nc.vector.tensor_tensor(feat[:].rearrange("p (c t) -> p c t", t=PACK), x, gain_rows[b][:], ALU.mult)
-            return feat
-
         def quantise_h(feat, b, c0, c1):
             nc.vector.quantize_mx(h_w[b][:, c0:c1].bitcast(FP8X4), h_s[b][:, c0:c1], feat)
 
-        def plane_relu(x_sum, name):
-            x = keep.tile([P, PACK * P], F32, name=name)
-            nc.scalar.activation(x[:], x_sum[:], ACT.Relu)
-            return x
+        def pair_passes(sums, b, piece, a, first, last, slices=range(PACK)):
+            cols = slice(WIDTH * piece, WIDTH * (piece + 1))
+            part, start = divmod(WIDTH * piece, S // GATHER_PARTS[a])
+            for i, t in enumerate(slices):
+                rows = slice(P * t, P * (t + 1))
+                nc.tensor.matmul_mx(
+                    sums[t // 2][:, WIDTH * (t % 2) : WIDTH * (t % 2 + 1)],
+                    lhsT=w1_w[b, a][:, rows].bitcast(FP8X4),
+                    lhsT_scale=w1_s[b, a][:, rows],
+                    rhs=v_w[a][part][:, start : start + WIDTH].bitcast(FP8X4),
+                    rhs_scale=v_s[4 * (a + 1) : P, cols],
+                    start=(first and i % 2 == 0),
+                    stop=(last and i % 2 == 1),
+                )
 
-        def plane_log(x):
-            nc.scalar.activation(x[:], x[:], ACT.Ln, bias=1.0)
+        def pair_product(b, piece, banks, order):
+            sums = [bank(i) for i in banks]
+            for i, a in enumerate(order):
+                pair_passes(sums, b, piece, a, i == 0, i == KA - 1, (3, 2, 1, 0))
+            return sums
 
-        def plane_gain(x, b, name):
-            planes = keep.tile([P, PACK, P], BF16, name=name)
+        def plane_relu(x_sum, x):
+            nc.scalar.activation(x, x_sum[:], ACT.Relu)
+
+        def plane_log(dst, src):
+            nc.scalar.activation(dst, src, ACT.Ln, bias=1.0)
+
+        def plane_gains(xs, b, piece):
+            planes = keep.tile([P, PACK, WIDTH], BF16, name=f"planes{b}")
             for t in range(PACK):
-                nc.scalar.activation(planes[:, t, :], x[:, P * t : P * (t + 1)], ACT.Copy, scale=gains[:, b, t : t + 1])
+                src = xs[t // 2][:, WIDTH * (t % 2) : WIDTH * (t % 2 + 1)]
+                nc.scalar.activation(planes[:, t, :], src, ACT.Copy, scale=gains[:, b, t : t + 1])
             return planes
 
-        def weave(feat, i, planes):
+        def weave(planes, b, piece, home=None):
+            if home:
+                feat = keep.tile([P, 2 * PASS], BF16, name=home, align_bytes=64)
+            else:
+                feat = stage.tile([P, 2 * PASS], BF16, name="feat", align_bytes=64)
             nc.scalar.copy(
-                feat[:, PASS * i : PASS * (i + 1)].rearrange("p (c e t) -> p c t e", e=PACK, t=PACK),
+                feat[:].rearrange("p (c e t) -> p c t e", e=PACK, t=PACK),
                 planes[:].rearrange("p t (c e) -> p c t e", e=PACK),
             )
-
-        def finish_pair(xs, b, piece, home="planes"):
-            planes = [plane_gain(x, b, f"{home}{i}") for i, x in enumerate(xs)]
-            feat = keep.tile([P, 2 * PASS], BF16, name=f"feat{b}{piece}", align_bytes=64)
-            for i in range(2):
-                weave(feat, i, planes[i])
             quantise_h(feat[:], b, WIDTH * piece, WIDTH * (piece + 1))
             return feat
 
@@ -207,64 +216,84 @@ def tile_list_posting_term_expansion_kernel(
         y_tiles = {}
         y_count = []
 
-        def expansion(piece, n, pieces=1):
+        def second_product(n, start, width):
+            y_sum = bank(2 + len(y_count) if len(y_count) < 2 else (0, 1, 4, 5)[len(y_count) % 4])
+            y_count.append(n)
+            cuts = [start, start + width % WIDTH, start + width] if width > WIDTH and width % WIDTH else [start, start + width]
+            for c0, c1 in zip(cuts, cuts[1:]):
+                for b in range(HB):
+                    nc.tensor.matmul_mx(
+                        y_sum[:, c0 - start : c1 - start],
+                        lhsT=w4_bytes[:, b, 2 * P * n : 2 * P * (n + 1)].bitcast(FP4X4),
+                        lhsT_scale=w4_scale_bytes[:, b, P * n : P * (n + 1)],
+                        rhs=h_w[b][:, c0:c1].bitcast(FP8X4),
+                        rhs_scale=h_s[b][:, c0:c1],
+                        start=(b == 0),
+                        stop=(b == HB - 1),
+                    )
+            return y_sum[:, :width]
+
+        def window(n, start, width):
+            return cache[n][:].indirect(places[:, start // LIST : (start + width) // LIST])
+
+        def opening_product(n, home):
+            weighted = keep.tile([P, P], F32, name=home, align_bytes=64)
+            nc.vector.scalar_tensor_tensor(weighted[:], second_product(n, 0, P), 0.0, weights[:, :P], ALU.max, ALU.mult)
+            return weighted
+
+        def opening_scatter(n, weighted):
+            nc.vector.tensor_tensor(window(n, 0, P), weighted[:], zeros[:], ALU.add)
+
+        def expansion(piece, n, pieces=1, home=None):
             start, width = WIDTH * piece, WIDTH * pieces
-            if pieces > 1:
+            if piece == 1 and n < 2:
+                start, width = P, P + WIDTH
+                y = keep.tile([P, width], F32, name=f"x0{n}")[:]
+            elif home:
+                y = keep.tile([P, width], F32, name=home)[:]
+            elif pieces > 1:
                 y = keep.tile([P, width], F32, name=f"x0{n - 4}")[:]
             else:
                 if piece not in y_tiles:
                     y_tiles[piece] = keep.tile([P, NT, WIDTH], F32, name=f"raw{(piece + 2) % 4}")
                 y = y_tiles[piece][:, n, :]
-            y_sum = bank(6 + len(y_count) % 2)
-            y_count.append(n)
-            for c0 in range(0, width, P):
-                for b in range(HB):
-                    nc.tensor.matmul_mx(
-                        y_sum[:, c0 : c0 + P],
-                        lhsT=w4_bytes[:, b, 2 * P * n : 2 * P * (n + 1)].bitcast(FP4X4),
-                        lhsT_scale=w4_scale_bytes[:, b, P * n : P * (n + 1)],
-                        rhs=h_w[b][:, start + c0 : start + c0 + P].bitcast(FP8X4),
-                        rhs_scale=h_s[b][:, start + c0 : start + c0 + P],
-                        start=(b == 0),
-                        stop=(b == HB - 1),
-                    )
-            nc.scalar.activation(y, y_sum[:, :width], ACT.Relu)
-            nc.vector.tensor_tensor(
-                cache[n][:].indirect(places[:, start // LIST : (start + width) // LIST]),
-                y,
-                weights[:, start : start + width],
-                ALU.mult,
-            )
+            nc.scalar.activation(y, second_product(n, start, width), ACT.Relu)
+            nc.vector.tensor_tensor(window(n, start, width), y, weights[:, start : start + width], ALU.mult)
             if start + width == S:
                 nc.sync.dma_start(out[P * n : P * (n + 1), :], cache[n][:])
 
-        def plane_pair(b, piece, banks, between):
-            sums = [first_product(b, 2 * piece + i, banks[i]) for i in range(2)]
-            xs = [plane_relu(sums[i], f"xp{i}") for i in range(2)]
-            for step in between[:1]:
-                expansion(*step)
-            for x in xs:
-                plane_log(x)
-            for step in between[1:]:
-                expansion(*step)
-            return finish_pair(xs, b, piece)
+        def halves_of(name):
+            both = keep.tile([P, 2, BANK], F32, name=name)
+            return [both[:, i] for i in range(2)]
 
         gather(v_w[0], tab_w[0][:].bitcast(U32))
         gather([v_s], tab_s[:].bitcast(U8))
-        early = [bank(i) for i in (0, 1, 2, 3, 6, 7)]
+        early = [bank(i) for i in range(2)]
+        second_pair = [bank(i) for i in (2, 3)]
+        ahead = [bank(i) for i in (6, 7)]
         for a in range(KA):
             quantise_w1(0, a, [("scalar", 0, P)], PASS)
             if a > 0:
                 gather(v_w[a], tab_w[a][:].bitcast(U32))
-            for u in range(6):
+            for u in range(2):
                 first_passes(early[u], 0, a, u)
+            pair_passes(second_pair, 0, 1, a, a == 0, a == KA - 1)
+            pair_passes(ahead, 0, 2, a, a == 0, a == KA - 1)
+
+        opening = keep.tile([P, P, PACK], F32, name="x00")
+        woven = early[0][:].rearrange("p (t c) -> p c t", t=PACK)
+        nc.vector.tensor_scalar_max(opening[:, :LIST], woven[:, :LIST], 0.0)
+        woven_log(opening[:, :LIST])
 
         lead = [bank(4 + u) for u in range(2)]
         for a in range(KA - 1):
             quantise_w1(1, a, [("vector", 0, P)], PASS)
             for u in range(2):
                 first_passes(lead[u], 1, a, u)
-        x0 = [woven_log(woven_relu(early[u], f"x0{u}")) for u in range(2)]
+        nc.scalar.activation(opening[:, LIST:], woven[:, LIST:], ACT.Relu)
+        x0 = [opening[:], woven_relu(early[1], "x01")]
+        woven_log(opening[:, LIST:])
+        woven_log(x0[1])
         quantise_w1(1, KA - 1, [("vector", 0, P)], 2 * P)
         for slices in ((0, 1), (2, 3)):
             for u in range(2):
@@ -278,40 +307,84 @@ def tile_list_posting_term_expansion_kernel(
                 )
             for half in halves:
                 woven_log(x1[u][:, half])
-        x0.extend(woven_relu(early[u], f"x0{u}") for u in (2, 3))
-        for u in (2, 3):
-            woven_log(x0[u])
-        feat = keep.tile([P, 3, P, PACK], BF16, name="last_grouped", align_bytes=64)
-        for u in range(3):
+        x01 = halves_of("second")
+        for i in range(2):
+            plane_relu(second_pair[i], x01[i])
+        for x in x01:
+            plane_log(x, x)
+        planes = plane_gains(x01, 0, 1)
+        x02 = halves_of("ahead")
+        for i in range(2):
+            plane_relu(ahead[i], x02[i])
+        feat = keep.tile([P, 2, P, PACK], BF16, name="last_grouped", align_bytes=64)
+        for u in range(2):
             nc.vector.tensor_tensor(feat[:, u], x0[u], gain_rows[0][:], ALU.mult)
-        first = woven_gain(x1[0][:], 1, "feat1w0")
+        first = keep.tile([P, P, PACK], BF16, name="feat1w0", align_bytes=64)
+        for half in halves:
+            nc.vector.tensor_tensor(first[:, half], x1[0][:, half], gain_rows[1][:, half], ALU.mult)
         quantise_h(feat[:, 0:2].rearrange("p u c t -> p (u c t)"), 0, 0, 2 * P)
-        quantise_h(first[:], 1, 0, P)
+        quantise_h(first[:].rearrange("p c t -> p (c t)"), 1, 0, P)
         second = keep.tile([P, P, PACK], BF16, name="feat1w1", align_bytes=64)
-        for c0 in (0, P // 2):
-            half = slice(c0, c0 + P // 2)
+        for half in halves:
             nc.vector.tensor_tensor(second[:, half], x1[1][:, half], gain_rows[1][:, half], ALU.mult)
-        quantise_h(feat[:, 2].rearrange("p c t -> p (c t)"), 0, 2 * P, 3 * P)
+        weighted = [opening_product(0, "weighted0")]
         quantise_h(second[:].rearrange("p c t -> p (c t)"), 1, P, 2 * P)
-        quantise_h(woven_gain(x0[3], 0, "feat1w1")[:], 0, 3 * P, 4 * P)
-        expansion(0, 0)
-        expansion(0, 1)
-        ahead = [plane_relu(early[4 + i], f"xa{i}") for i in range(2)]
-        for x in ahead:
-            plane_log(x)
-        plane_pair(1, 1, [0, 1], [(0, 2), (0, 3)])
+        weighted.append(opening_product(1, "weighted1"))
+        for n in range(2):
+            opening_scatter(n, weighted[n])
+        sums = pair_product(1, 1, [0, 1], (0, 1, 2))
+        x11 = halves_of("x10")
+        for i in range(2):
+            plane_relu(sums[i], x11[i])
+        expansion(0, 2)
+        expansion(0, 3)
+        for x in x11:
+            plane_log(x, x)
+        f01 = weave(planes, 0, 1, "feat1w0")
         expansion(0, 4)
+        planes = plane_gains(x11, 1, 1)
+        logs = halves_of("x11")
+        plane_log(logs[0], x02[0])
+        f11 = weave(planes, 1, 1)
         expansion(0, 5)
-        finish_pair(ahead, 0, 2, "x1")
+        plane_log(logs[1], x02[1])
+        planes = plane_gains(logs, 0, 2)
         expansion(1, 0)
+        f02 = weave(planes, 0, 2)
         expansion(1, 1)
-        plane_pair(1, 2, [2, 3], [(1, 2), (1, 3)])
-        expansion(1, 4)
-        expansion(1, 5)
-        plane_pair(0, 3, [4, 5], [])
+
+        sums = pair_product(1, 2, [6, 7], (2, 0, 1))
+        x12 = halves_of("ahead")
+        for i in range(2):
+            plane_relu(sums[i], x12[i])
+        expansion(1, 2)
+        for x in x12:
+            plane_log(x, x)
+        planes = plane_gains(x12, 1, 2)
+        expansion(1, 3)
+        f12 = weave(planes, 1, 2)
+
+        sums = pair_product(0, 3, [2, 3], (0, 1, 2))
+        x03 = halves_of("x10")
+        for i in range(2):
+            plane_relu(sums[i], x03[i])
+            expansion(1, 4 + i)
+        for x in x03:
+            plane_log(x, x)
+        planes = plane_gains(x03, 0, 3)
         expansion(2, 0)
-        plane_pair(1, 3, [0, 1], [(2, 1), (2, 2)])
-        expansion(2, 3)
+        f03 = weave(planes, 0, 3)
+        sums = pair_product(1, 3, [6, 7], (0, 1, 2))
+        x13 = halves_of("x11")
+        for i in range(2):
+            plane_relu(sums[i], x13[i])
+        expansion(2, 1)
+        for x in x13:
+            plane_log(x, x)
+        planes = plane_gains(x13, 1, 3)
+        expansion(2, 2)
+        f13 = weave(planes, 1, 3)
+        expansion(2, 3, home="planes1")
         for n in range(4):
             expansion(3, n)
         for n in range(4, NT):

@@ -121,7 +121,10 @@ def tile_list_posting_term_expansion_kernel(
                 if engine == "scalar":
                     nc.scalar.activation(dst[:, m0:m1], src[:, m0:m1], ACT.Copy)
                 else:
-                    nc.vector.tensor_copy(dst[:, m0:m1], src[:, m0:m1])
+                    nc.vector.tensor_copy(
+                        grouped[:].rearrange("p (t m j) -> p m j t", t=PACK, j=PACK)[:, m0:m1],
+                        raw[b, a][:].rearrange("p j (m t) -> p m j t", t=PACK)[:, m0:m1],
+                    )
             w1_w[b, a] = keep.tile([P, PASS], U32, name=f"w1_w{b}{a}", align_bytes=64)
             w1_s[b, a] = keep.tile([P, PASS], U8, name=f"w1_s{b}{a}", align_bytes=64)
             for c0 in range(0, PASS, quantise_width):
@@ -137,7 +140,7 @@ def tile_list_posting_term_expansion_kernel(
         def first_passes(x_sum, b, a, u, slices=range(PACK)):
             cols = slice(P * u, P * (u + 1))
             part, first = divmod(P * u, S // GATHER_PARTS[a])
-            for t in slices:
+            for i, t in enumerate(slices):
                 rows = slice(P * t, P * (t + 1))
                 nc.tensor.matmul_mx(
                     x_sum[:, rows],
@@ -145,8 +148,8 @@ def tile_list_posting_term_expansion_kernel(
                     lhsT_scale=w1_s[b, a][:, rows],
                     rhs=v_w[a][part][:, first : first + P].bitcast(FP8X4),
                     rhs_scale=v_s[4 * (a + 1) : P, cols],
-                    start=(a == 0 and t == 0),
-                    stop=(a == KA - 1 and t == PACK - 1),
+                    start=(a == 0 and i == 0),
+                    stop=(a == KA - 1 and i == PACK - 1),
                 )
 
         h_w = [keep.tile([P, S], U32, name=f"h_w{b}", align_bytes=64) for b in range(HB)]
@@ -295,9 +298,8 @@ def tile_list_posting_term_expansion_kernel(
         woven_log(opening[:, LIST:])
         woven_log(x0[1])
         quantise_w1(1, KA - 1, [("vector", 0, P)], 2 * P)
-        for slices in ((0, 1), (2, 3)):
-            for u in range(2):
-                first_passes(lead[u], 1, KA - 1, u, slices)
+        first_passes(lead[0], 1, KA - 1, 0)
+        first_passes(lead[1], 1, KA - 1, 1, (3, 2, 1, 0))
         halves = [slice(c0, c0 + P // 2) for c0 in (0, P // 2)]
         x1 = [keep.tile([P, P, PACK], F32, name=f"x1{u}") for u in range(2)]
         for u in range(2):

@@ -23,7 +23,7 @@ HB = H // PASS
 NT = N // P
 BANK = 512
 WIDTH = 256
-GATHER_PARTS = (1, 1, 2)
+GATHER_CUTS = ((0, S), (0, S), (0, 2 * WIDTH, S))
 LIST = 16
 
 
@@ -34,16 +34,18 @@ def tile_list_posting_term_expansion_kernel(
     with ExitStack() as ctx:
         keep = ctx.enter_context(tc.tile_pool(name="keep", bufs=1))
         stage = ctx.enter_context(tc.tile_pool(name="stage", bufs=2))
+        shared = ctx.enter_context(tc.tile_pool(name="shared", bufs=1))
         psum = ctx.enter_context(tc.psum_pool(name="psum", bufs=1))
 
         picks = keep.tile([P, S // LIST], U16, name="picks")
         places = keep.tile([P, S // LIST], U16, name="places")
         tab_w = [keep.tile([P, T], I32, name=f"tab_w{a}", align_bytes=64) for a in range(KA)]
         tab_s = keep.tile([P, T // 4], I32, name="tab_s", align_bytes=64)
-        v_w = [
-            [keep.tile([P, S // parts], U32, name=f"v_w{a}{i}", align_bytes=64) for i in range(parts)]
-            for a, parts in enumerate(GATHER_PARTS)
-        ]
+        v_w = {
+            (a, c0): keep.tile([P, c1 - c0], U32, name=f"v_w{a}_{c0}", align_bytes=64)
+            for a, cuts in enumerate(GATHER_CUTS)
+            for c0, c1 in zip(cuts, cuts[1:])
+        }
         v_s = keep.tile([P, S], U8, name="v_s", align_bytes=64)
         w4_w = keep.tile([P, HB, 2 * N // 4], I32, name="w4_w", align_bytes=64)
         w4_s = keep.tile([P, HB, N // 4], I32, name="w4_s", align_bytes=64)
@@ -52,15 +54,33 @@ def tile_list_posting_term_expansion_kernel(
         weights = keep.tile([P, S], F32, name="weights")
         cache = [keep.tile([P, T2], F32, name=f"cache{n}") for n in range(NT)]
 
+        def scale_loads(queue):
+            for q in range(4):
+                queue.dma_start(
+                    tab_s[32 * q + 4 : 32 * q + 4 + 4 * KA, :], tab_scales[:, 4 * q : 4 * q + 4, :].bitcast(I32)
+                )
+
+        def load_table(a):
+            nc.sync.dma_start(tab_w[a][:], tab_words[a].rearrange("p t i -> p (t i)").bitcast(I32))
+
+        def gain_load(queue):
+            queue.dma_start(gains[:], gain.rearrange("(b p t) -> p b t", b=HB, t=PACK))
+
+        def gather_words(a):
+            cuts = GATHER_CUTS[a]
+            for c0, c1 in zip(cuts, cuts[1:]):
+                window = tab_w[a][:].bitcast(U32)
+                nc.vector.tensor_copy(v_w[a, c0][:], window.indirect(picks[:, c0 // LIST : c1 // LIST]))
+
+        def picked(a, start, width):
+            c0 = max(c for c in GATHER_CUTS[a] if c <= start)
+            return v_w[a, c0][:, start - c0 : start - c0 + width].bitcast(FP8X4)
+
         nc.gpsimd.memset(tab_s[:], 0)
-        for q in range(4):
-            nc.gpsimd.dma_start(
-                tab_s[32 * q + 4 : 32 * q + 4 + 4 * KA, :], tab_scales[:, 4 * q : 4 * q + 4, :].bitcast(I32)
-            )
+        scale_loads(nc.gpsimd)
         nc.vector.memset(w4_s[:], 0)
         zeros = keep.tile([P, P], F32, name="zeros")
-        nc.vector.memset(zeros[:], 0.0)
-        nc.gpsimd.dma_start(gains[:], gain.rearrange("(b p t) -> p b t", b=HB, t=PACK))
+        gain_load(nc.gpsimd)
         for n in range(NT):
             if n < 4:
                 nc.vector.memset(cache[n][:, : T2 // 2 - 1], 0.0)
@@ -72,9 +92,6 @@ def tile_list_posting_term_expansion_kernel(
                 w4_s[32 * q : 32 * q + 4, :, :],
                 w4_scales[:, 4 * q : 4 * q + 4, :].rearrange("b r n -> r b n").bitcast(I32),
             )
-
-        def load_table(a):
-            nc.sync.dma_start(tab_w[a][:], tab_words[a].rearrange("p t i -> p (t i)").bitcast(I32))
 
         load_table(0)
         nc.sync.dma_start(picks[:], offs)
@@ -103,16 +120,11 @@ def tile_list_posting_term_expansion_kernel(
         for b in range(HB):
             nc.scalar.copy(gain_rows[b][:], gains[:, b, :].unsqueeze(1).to_broadcast([P, P, PACK]))
 
-        def gather(parts, window):
-            count = S // len(parts) // LIST
-            for i, part in enumerate(parts):
-                nc.vector.tensor_copy(part[:], window.indirect(picks[:, count * i : count * (i + 1)]))
-
         w1_w, w1_s = {}, {}
 
         def quantise_w1(b, a, shares, quantise_width):
             if (b, a) == (HB - 1, KA - 1):
-                grouped = keep.tile([P, PACK * PASS], BF16, name="last_grouped", align_bytes=64)
+                grouped = shared.tile([P, PACK * PASS], BF16, name="last_grouped", align_bytes=64, offset=0)
             else:
                 grouped = stage.tile([P, PACK * PASS], BF16, name="grouped", align_bytes=64)
             dst = grouped[:].rearrange("p (t m j) -> p m t j", t=PACK, j=PACK)
@@ -125,6 +137,8 @@ def tile_list_posting_term_expansion_kernel(
                         grouped[:].rearrange("p (t m j) -> p m j t", t=PACK, j=PACK)[:, m0:m1],
                         raw[b, a][:].rearrange("p j (m t) -> p m j t", t=PACK)[:, m0:m1],
                     )
+            if (b, a) == (0, KA - 1):
+                nc.scalar.activation(zeros[:], grouped[:, :P], ACT.Ln, bias=1.0, scale=0.0)
             w1_w[b, a] = keep.tile([P, PASS], U32, name=f"w1_w{b}{a}", align_bytes=64)
             w1_s[b, a] = keep.tile([P, PASS], U8, name=f"w1_s{b}{a}", align_bytes=64)
             for c0 in range(0, PASS, quantise_width):
@@ -139,14 +153,13 @@ def tile_list_posting_term_expansion_kernel(
 
         def first_passes(x_sum, b, a, u, slices=range(PACK)):
             cols = slice(P * u, P * (u + 1))
-            part, first = divmod(P * u, S // GATHER_PARTS[a])
             for i, t in enumerate(slices):
                 rows = slice(P * t, P * (t + 1))
                 nc.tensor.matmul_mx(
                     x_sum[:, rows],
                     lhsT=w1_w[b, a][:, rows].bitcast(FP8X4),
                     lhsT_scale=w1_s[b, a][:, rows],
-                    rhs=v_w[a][part][:, first : first + P].bitcast(FP8X4),
+                    rhs=picked(a, P * u, P),
                     rhs_scale=v_s[4 * (a + 1) : P, cols],
                     start=(a == 0 and i == 0),
                     stop=(a == KA - 1 and i == PACK - 1),
@@ -154,6 +167,13 @@ def tile_list_posting_term_expansion_kernel(
 
         h_w = [keep.tile([P, S], U32, name=f"h_w{b}", align_bytes=64) for b in range(HB)]
         h_s = [keep.tile([P, S], U8, name=f"h_s{b}", align_bytes=64) for b in range(HB)]
+
+        held_s = shared.tile([P, WIDTH], U8, name="held_s", align_bytes=64, offset=4 * PASS)
+
+        def h_scales(b, c0, c1):
+            if b == 0 and c0 // WIDTH == 1:
+                return held_s[:, c0 - WIDTH : c1 - WIDTH]
+            return h_s[b][:, c0:c1]
 
         def woven_relu(x_sum, name):
             x = keep.tile([P, P, PACK], F32, name=name)[:]
@@ -165,18 +185,17 @@ def tile_list_posting_term_expansion_kernel(
             return x
 
         def quantise_h(feat, b, c0, c1):
-            nc.vector.quantize_mx(h_w[b][:, c0:c1].bitcast(FP8X4), h_s[b][:, c0:c1], feat)
+            nc.vector.quantize_mx(h_w[b][:, c0:c1].bitcast(FP8X4), h_scales(b, c0, c1), feat)
 
         def pair_passes(sums, b, piece, a, first, last, slices=range(PACK)):
             cols = slice(WIDTH * piece, WIDTH * (piece + 1))
-            part, start = divmod(WIDTH * piece, S // GATHER_PARTS[a])
             for i, t in enumerate(slices):
                 rows = slice(P * t, P * (t + 1))
                 nc.tensor.matmul_mx(
                     sums[t // 2][:, WIDTH * (t % 2) : WIDTH * (t % 2 + 1)],
                     lhsT=w1_w[b, a][:, rows].bitcast(FP8X4),
                     lhsT_scale=w1_s[b, a][:, rows],
-                    rhs=v_w[a][part][:, start : start + WIDTH].bitcast(FP8X4),
+                    rhs=picked(a, WIDTH * piece, WIDTH),
                     rhs_scale=v_s[4 * (a + 1) : P, cols],
                     start=(first and i % 2 == 0),
                     stop=(last and i % 2 == 1),
@@ -201,15 +220,15 @@ def tile_list_posting_term_expansion_kernel(
                 nc.scalar.activation(planes[:, t, :], src, ACT.Copy, scale=gains[:, b, t : t + 1])
             return planes
 
-        def weave(planes, b, piece, home=None):
-            if home:
-                feat = keep.tile([P, 2 * PASS], BF16, name=home, align_bytes=64)
-            else:
-                feat = stage.tile([P, 2 * PASS], BF16, name="feat", align_bytes=64)
+        def interleave(feat, planes):
             nc.scalar.copy(
                 feat[:].rearrange("p (c e t) -> p c t e", e=PACK, t=PACK),
                 planes[:].rearrange("p t (c e) -> p c t e", e=PACK),
             )
+
+        def weave(planes, b, piece):
+            feat = stage.tile([P, 2 * PASS], BF16, name="feat", align_bytes=64)
+            interleave(feat, planes)
             quantise_h(feat[:], b, WIDTH * piece, WIDTH * (piece + 1))
             return feat
 
@@ -230,7 +249,7 @@ def tile_list_posting_term_expansion_kernel(
                         lhsT=w4_bytes[:, b, 2 * P * n : 2 * P * (n + 1)].bitcast(FP4X4),
                         lhsT_scale=w4_scale_bytes[:, b, P * n : P * (n + 1)],
                         rhs=h_w[b][:, c0:c1].bitcast(FP8X4),
-                        rhs_scale=h_s[b][:, c0:c1],
+                        rhs_scale=h_scales(b, c0, c1),
                         start=(b == 0),
                         stop=(b == HB - 1),
                     )
@@ -269,56 +288,53 @@ def tile_list_posting_term_expansion_kernel(
             both = keep.tile([P, 2, BANK], F32, name=name)
             return [both[:, i] for i in range(2)]
 
-        gather(v_w[0], tab_w[0][:].bitcast(U32))
-        gather([v_s], tab_s[:].bitcast(U8))
+        gather_words(0)
+        nc.vector.tensor_copy(v_s[:], tab_s[:].bitcast(U8).indirect(picks[:]))
         early = [bank(i) for i in range(2)]
         second_pair = [bank(i) for i in (2, 3)]
         ahead = [bank(i) for i in (6, 7)]
         for a in range(KA):
             quantise_w1(0, a, [("scalar", 0, P)], PASS)
             if a > 0:
-                gather(v_w[a], tab_w[a][:].bitcast(U32))
+                gather_words(a)
             for u in range(2):
                 first_passes(early[u], 0, a, u)
             pair_passes(second_pair, 0, 1, a, a == 0, a == KA - 1)
             pair_passes(ahead, 0, 2, a, a == 0, a == KA - 1)
 
-        opening = keep.tile([P, P, PACK], F32, name="x00")
-        woven = early[0][:].rearrange("p (t c) -> p c t", t=PACK)
-        nc.vector.tensor_scalar_max(opening[:, :LIST], woven[:, :LIST], 0.0)
-        woven_log(opening[:, :LIST])
+        x0 = [woven_relu(early[u], f"x0{u}") for u in range(2)]
+        for u in range(2):
+            woven_log(x0[u])
 
         lead = [bank(4 + u) for u in range(2)]
         for a in range(KA - 1):
             quantise_w1(1, a, [("vector", 0, P)], PASS)
             for u in range(2):
                 first_passes(lead[u], 1, a, u)
-        nc.scalar.activation(opening[:, LIST:], woven[:, LIST:], ACT.Relu)
-        x0 = [opening[:], woven_relu(early[1], "x01")]
-        woven_log(opening[:, LIST:])
-        woven_log(x0[1])
         quantise_w1(1, KA - 1, [("vector", 0, P)], 2 * P)
         first_passes(lead[0], 1, KA - 1, 0)
         first_passes(lead[1], 1, KA - 1, 1, (3, 2, 1, 0))
         halves = [slice(c0, c0 + P // 2) for c0 in (0, P // 2)]
         x1 = [keep.tile([P, P, PACK], F32, name=f"x1{u}") for u in range(2)]
+        cut = [x1[0], keep.tile([P, P, PACK], F32, name="lead_cut")]
         for u in range(2):
             for half in halves:
                 nc.scalar.activation(
-                    x1[u][:, half], lead[u][:].rearrange("p (t c) -> p c t", t=PACK)[:, half], ACT.Relu
+                    cut[u][:, half], lead[u][:].rearrange("p (t c) -> p c t", t=PACK)[:, half], ACT.Relu
                 )
             for half in halves:
-                woven_log(x1[u][:, half])
+                plane_log(x1[u][:, half], cut[u][:, half])
         x01 = halves_of("second")
         for i in range(2):
             plane_relu(second_pair[i], x01[i])
         for x in x01:
             plane_log(x, x)
         planes = plane_gains(x01, 0, 1)
-        x02 = halves_of("ahead")
-        for i in range(2):
-            plane_relu(ahead[i], x02[i])
-        feat = keep.tile([P, 2, P, PACK], BF16, name="last_grouped", align_bytes=64)
+        x02 = [keep.tile([P, BANK], F32, name="ahead")[:], keep.tile([P, BANK], F32, name="lead_cut")[:]]
+        early_feat = stage.tile([P, 2 * PASS], BF16, name="feat", align_bytes=64)
+        interleave(early_feat, planes)
+        plane_relu(ahead[0], x02[0])
+        feat = shared.tile([P, 2, P, PACK], BF16, name="opening_feat", align_bytes=64, offset=0)
         for u in range(2):
             nc.vector.tensor_tensor(feat[:, u], x0[u], gain_rows[0][:], ALU.mult)
         first = keep.tile([P, P, PACK], BF16, name="feat1w0", align_bytes=64)
@@ -334,6 +350,7 @@ def tile_list_posting_term_expansion_kernel(
         weighted.append(opening_product(1, "weighted1"))
         for n in range(2):
             opening_scatter(n, weighted[n])
+        quantise_h(early_feat[:], 0, WIDTH, 2 * WIDTH)
         sums = pair_product(1, 1, [0, 1], (0, 1, 2))
         x11 = halves_of("x10")
         for i in range(2):
@@ -342,7 +359,7 @@ def tile_list_posting_term_expansion_kernel(
         expansion(0, 3)
         for x in x11:
             plane_log(x, x)
-        f01 = weave(planes, 0, 1, "feat1w0")
+        plane_relu(ahead[1], x02[1])
         expansion(0, 4)
         planes = plane_gains(x11, 1, 1)
         logs = halves_of("x11")

@@ -222,8 +222,8 @@ def tile_list_posting_term_expansion_kernel(
 
         def interleave(feat, planes):
             nc.scalar.copy(
-                feat[:].rearrange("p (c e t) -> p c t e", e=PACK, t=PACK),
-                planes[:].rearrange("p t (c e) -> p c t e", e=PACK),
+                feat[:].rearrange("p (c e t) -> p c t e", e=2 * PACK, t=PACK),
+                planes[:].rearrange("p t (c e) -> p c t e", e=2 * PACK),
             )
 
         def weave(planes, b, piece):
@@ -282,7 +282,10 @@ def tile_list_posting_term_expansion_kernel(
             nc.scalar.activation(y, second_product(n, start, width), ACT.Relu)
             nc.vector.tensor_tensor(window(n, start, width), y, weights[:, start : start + width], ALU.mult)
             if start + width == S:
-                nc.sync.dma_start(out[P * n : P * (n + 1), :], cache[n][:])
+                queues = (nc.sync, nc.scalar) if n == NT - 1 else (nc.sync,)
+                for i, queue in enumerate(queues):
+                    cols = slice(i * T2 // len(queues), (i + 1) * T2 // len(queues))
+                    queue.dma_start(out[P * n : P * (n + 1), cols], cache[n][:, cols])
 
         def halves_of(name):
             both = keep.tile([P, 2, BANK], F32, name=name)

@@ -87,12 +87,6 @@ def tile_list_posting_term_expansion_kernel(
                 nc.vector.memset(cache[n][:, T2 // 2 - 1 :], 0.0)
             else:
                 nc.gpsimd.memset(cache[n][:], 0.0)
-        for q in range(4):
-            nc.gpsimd.dma_start(
-                w4_s[32 * q : 32 * q + 4, :, :],
-                w4_scales[:, 4 * q : 4 * q + 4, :].rearrange("b r n -> r b n").bitcast(I32),
-            )
-
         load_table(0)
         nc.sync.dma_start(picks[:], offs)
 
@@ -114,6 +108,11 @@ def tile_list_posting_term_expansion_kernel(
         load_w1(1, 1)
         load_w1(1, 2)
         nc.sync.dma_start(w4_w[:], w4_words.rearrange("b p c -> p b c").bitcast(I32))
+        for q in range(4):
+            nc.sync.dma_start(
+                w4_s[32 * q : 32 * q + 4, :, :],
+                w4_scales[:, 4 * q : 4 * q + 4, :].rearrange("b r n -> r b n").bitcast(I32),
+            )
         nc.sync.dma_start(places[:], offs2)
         nc.sync.dma_start(weights[:], wgo)
 

from contextlib import ExitStack

import concourse.mybir as mybir

K, H, N, T, S, T2, P = 1536, 1024, 768, 4096, 1024, 2048, 128
FLOPS = 2 * K * H * S + 2 * H * N * S

F32 = mybir.dt.float32
BF16 = mybir.dt.bfloat16
I32 = mybir.dt.int32
U32 = mybir.dt.uint32
U16 = mybir.dt.uint16
U8 = mybir.dt.uint8
FP8X4 = mybir.dt.float8_e4m3fn_x4
FP4X4 = mybir.dt.float4_e2m1fn_x4
ACT = mybir.ActivationFunctionType
ALU = mybir.AluOpType

PACK = 4
PASS = P * PACK
KA = K // PASS
HB = H // PASS
NT = N // P
BANK = 512
WIDTH = 256
GATHER_CUTS = ((0, S), (0, S), (0, 2 * WIDTH, S))
LIST = 16


def tile_list_posting_term_expansion_kernel(
    tc, tab_words, tab_scales, offs, w1, gain, w4_words, w4_scales, wgo, offs2, out
):
    nc = tc.nc
    with ExitStack() as ctx:
        keep = ctx.enter_context(tc.tile_pool(name="keep", bufs=1))
        stage = ctx.enter_context(tc.tile_pool(name="stage", bufs=2))
        shared = ctx.enter_context(tc.tile_pool(name="shared", bufs=1))
        psum = ctx.enter_context(tc.psum_pool(name="psum", bufs=1))

        picks = keep.tile([P, S // LIST], U16, name="picks")
        places = keep.tile([P, S // LIST], U16, name="places")
        tab_w = [keep.tile([P, T], I32, name=f"tab_w{a}", align_bytes=64) for a in range(KA)]
        tab_s = keep.tile([P, T // 4], I32, name="tab_s", align_bytes=64)
        v_w = {
            (a, c0): keep.tile([P, c1 - c0], U32, name=f"v_w{a}_{c0}", align_bytes=64)
            for a, cuts in enumerate(GATHER_CUTS)
            for c0, c1 in zip(cuts, cuts[1:])
        }
        v_s = keep.tile([P, S], U8, name="v_s", align_bytes=64)
        w4_w = keep.tile([P, HB, 2 * N // 4], I32, name="w4_w", align_bytes=64)
        w4_s = keep.tile([P, HB, N // 4], I32, name="w4_s", align_bytes=64)
        gains = keep.tile([P, HB, PACK], F32, name="gains")
        gain_rows = [keep.tile([P, P, PACK], F32, name=f"gain_rows{b}") for b in range(HB)]
        weights = keep.tile([P, S], F32, name="weights")
        cache = [keep.tile([P, T2], F32, name=f"cache{n}") for n in range(NT)]

        def scale_loads(queue):
            for q in range(4):
                queue.dma_start(
                    tab_s[32 * q + 4 : 32 * q + 4 + 4 * KA, :], tab_scales[:, 4 * q : 4 * q + 4, :].bitcast(I32)
                )

        def load_table(a):
            nc.sync.dma_start(tab_w[a][:], tab_words[a].rearrange("p t i -> p (t i)").bitcast(I32))

        def gain_load(queue):
            queue.dma_start(gains[:], gain.rearrange("(b p t) -> p b t", b=HB, t=PACK))

        def gather_words(a):
            cuts = GATHER_CUTS[a]
            for c0, c1 in zip(cuts, cuts[1:]):
                window = tab_w[a][:].bitcast(U32)
                nc.vector.tensor_copy(v_w[a, c0][:], window.indirect(picks[:, c0 // LIST : c1 // LIST]))

        def picked(a, start, width):
            c0 = max(c for c in GATHER_CUTS[a] if c <= start)
            return v_w[a, c0][:, start - c0 : start - c0 + width].bitcast(FP8X4)

        nc.gpsimd.memset(tab_s[:], 0)
        scale_loads(nc.gpsimd)
        nc.vector.memset(w4_s[:], 0)
        zeros = keep.tile([P, P], F32, name="zeros")
        gain_load(nc.gpsimd)
        for n in range(NT):
            if n < 4:
                nc.vector.memset(cache[n][:, : T2 // 2 - 1], 0.0)
                nc.vector.memset(cache[n][:, T2 // 2 - 1 :], 0.0)
            else:
                nc.gpsimd.memset(cache[n][:], 0.0)
        load_table(0)
        nc.sync.dma_start(picks[:], offs)

        raw = {}

        def load_w1(b, a, cuts=(0, PASS)):
            raw[b, a] = keep.tile([P, PACK, PASS], F32, name=f"raw{(KA * b + a) % 4}")
            block = w1[PASS * a : PASS * (a + 1), PASS * b : PASS * (b + 1)].rearrange("(p j) c -> p j c", j=PACK)
            for c0, c1 in zip(cuts, cuts[1:]):
                cols = slice(c0, c1)
                nc.sync.dma_start(raw[b, a][:, :, cols], block[:, :, cols])

        load_w1(0, 0)
        load_table(1)
        load_w1(0, 1)
        load_w1(0, 2)
        load_table(2)
        load_w1(1, 0)
        load_w1(1, 1)
        load_w1(1, 2)
        nc.sync.dma_start(w4_w[:], w4_words.rearrange("b p c -> p b c").bitcast(I32))
        for q in range(4):
            nc.sync.dma_start(
                w4_s[32 * q : 32 * q + 4, :, :],
                w4_scales[:, 4 * q : 4 * q + 4, :].rearrange("b r n -> r b n").bitcast(I32),
            )
        nc.sync.dma_start(places[:], offs2)
        nc.sync.dma_start(weights[:], wgo)

        for b in range(HB):
            nc.scalar.copy(gain_rows[b][:], gains[:, b, :].unsqueeze(1).to_broadcast([P, P, PACK]))

        w1_w, w1_s = {}, {}

        def quantise_w1(b, a, shares, quantise_width):
            if (b, a) == (HB - 1, KA - 1):
                grouped = shared.tile([P, PACK * PASS], BF16, name="last_grouped", align_bytes=64, offset=0)
            else:
                grouped = stage.tile([P, PACK * PASS], BF16, name="grouped", align_bytes=64)
            dst = grouped[:].rearrange("p (t m j) -> p m t j", t=PACK, j=PACK)
            src = raw[b, a][:].rearrange("p j (m t) -> p m t j", t=PACK)
            for engine, m0, m1 in shares:
                if engine == "scalar":
                    nc.scalar.activation(dst[:, m0:m1], src[:, m0:m1], ACT.Copy)
                else:
                    nc.vector.tensor_copy(
                        grouped[:].rearrange("p (t m j) -> p m j t", t=PACK, j=PACK)[:, m0:m1],
                        raw[b, a][:].rearrange("p j (m t) -> p m j t", t=PACK)[:, m0:m1],
                    )
            if (b, a) == (0, KA - 1):
                nc.scalar.activation(zeros[:], grouped[:, :P], ACT.Ln, bias=1.0, scale=0.0)
            w1_w[b, a] = keep.tile([P, PASS], U32, name=f"w1_w{b}{a}", align_bytes=64)
            w1_s[b, a] = keep.tile([P, PASS], U8, name=f"w1_s{b}{a}", align_bytes=64)
            for c0 in range(0, PASS, quantise_width):
                nc.vector.quantize_mx(
                    w1_w[b, a][:, c0 : c0 + quantise_width].bitcast(FP8X4),
                    w1_s[b, a][:, c0 : c0 + quantise_width],
                    grouped[:, PACK * c0 : PACK * (c0 + quantise_width)],
                )

        def bank(i):
            return psum.tile([P, BANK], F32, name=f"bank{i}")

        def first_passes(x_sum, b, a, u, slices=range(PACK)):
            cols = slice(P * u, P * (u + 1))
            for i, t in enumerate(slices):
                rows = slice(P * t, P * (t + 1))
                nc.tensor.matmul_mx(
                    x_sum[:, rows],
                    lhsT=w1_w[b, a][:, rows].bitcast(FP8X4),
                    lhsT_scale=w1_s[b, a][:, rows],
                    rhs=picked(a, P * u, P),
                    rhs_scale=v_s[4 * (a + 1) : P, cols],
                    start=(a == 0 and i == 0),
                    stop=(a == KA - 1 and i == PACK - 1),
                )

        h_w = [keep.tile([P, S], U32, name=f"h_w{b}", align_bytes=64) for b in range(HB)]
        h_s = [keep.tile([P, S], U8, name=f"h_s{b}", align_bytes=64) for b in range(HB)]

        held_s = shared.tile([P, WIDTH], U8, name="held_s", align_bytes=64, offset=4 * PASS)

        def h_scales(b, c0, c1):
            if b == 0 and c0 // WIDTH == 1:
                return held_s[:, c0 - WIDTH : c1 - WIDTH]
            return h_s[b][:, c0:c1]

        def woven_relu(x_sum, name):
            x = keep.tile([P, P, PACK], F32, name=name)[:]
            nc.scalar.activation(x, x_sum[:].rearrange("p (t c) -> p c t", t=PACK), ACT.Relu)
            return x

        def woven_log(x):
            nc.scalar.activation(x, x, ACT.Ln, bias=1.0)
            return x

        def quantise_h(feat, b, c0, c1):
            nc.vector.quantize_mx(h_w[b][:, c0:c1].bitcast(FP8X4), h_scales(b, c0, c1), feat)

        def pair_passes(sums, b, piece, a, first, last, slices=range(PACK)):
            cols = slice(WIDTH * piece, WIDTH * (piece + 1))
            for i, t in enumerate(slices):
                rows = slice(P * t, P * (t + 1))
                nc.tensor.matmul_mx(
                    sums[t // 2][:, WIDTH * (t % 2) : WIDTH * (t % 2 + 1)],
                    lhsT=w1_w[b, a][:, rows].bitcast(FP8X4),
                    lhsT_scale=w1_s[b, a][:, rows],
                    rhs=picked(a, WIDTH * piece, WIDTH),
                    rhs_scale=v_s[4 * (a + 1) : P, cols],
                    start=(first and i % 2 == 0),
                    stop=(last and i % 2 == 1),
                )

        def pair_product(b, piece, banks, order):
            sums = [bank(i) for i in banks]
            for i, a in enumerate(order):
                pair_passes(sums, b, piece, a, i == 0, i == KA - 1, (3, 2, 1, 0))
            return sums

        def plane_relu(x_sum, x):
            nc.scalar.activation(x, x_sum[:], ACT.Relu)

        def plane_log(dst, src):
            nc.scalar.activation(dst, src, ACT.Ln, bias=1.0)

        def plane_gains(xs, b, piece):
            planes = keep.tile([P, PACK, WIDTH], BF16, name=f"planes{b}")
            for t in range(PACK):
                src = xs[t // 2][:, WIDTH * (t % 2) : WIDTH * (t % 2 + 1)]
                nc.scalar.activation(planes[:, t, :], src, ACT.Copy, scale=gains[:, b, t : t + 1])
            return planes

        def interleave(feat, planes):
            nc.scalar.copy(
                feat[:].rearrange("p (c e t) -> p c t e", e=2 * PACK, t=PACK),
                planes[:].rearrange("p t (c e) -> p c t e", e=2 * PACK),
            )

        def weave(planes, b, piece):
            feat = stage.tile([P, 2 * PASS], BF16, name="feat", align_bytes=64)
            interleave(feat, planes)
            quantise_h(feat[:], b, WIDTH * piece, WIDTH * (piece + 1))
            return feat

        w4_bytes = w4_w[:].bitcast(U8)
        w4_scale_bytes = w4_s[:].bitcast(U8)

        y_tiles = {}
        y_count = []

        def second_product(n, start, width):
            y_sum = bank(2 + len(y_count) if len(y_count) < 2 else (0, 1, 4, 5)[len(y_count) % 4])
            y_count.append(n)
            cuts = [start, start + width % WIDTH, start + width] if width > WIDTH and width % WIDTH else [start, start + width]
            for c0, c1 in zip(cuts, cuts[1:]):
                for b in range(HB):
                    nc.tensor.matmul_mx(
                        y_sum[:, c0 - start : c1 - start],
                        lhsT=w4_bytes[:, b, 2 * P * n : 2 * P * (n + 1)].bitcast(FP4X4),
                        lhsT_scale=w4_scale_bytes[:, b, P * n : P * (n + 1)],
                        rhs=h_w[b][:, c0:c1].bitcast(FP8X4),
                        rhs_scale=h_scales(b, c0, c1),
                        start=(b == 0),
                        stop=(b == HB - 1),
                    )
            return y_sum[:, :width]

        def window(n, start, width):
            return cache[n][:].indirect(places[:, start // LIST : (start + width) // LIST])

        def opening_product(n, home):
            weighted = keep.tile([P, P], F32, name=home, align_bytes=64)
            nc.vector.scalar_tensor_tensor(weighted[:], second_product(n, 0, P), 0.0, weights[:, :P], ALU.max, ALU.mult)
            return weighted

        def opening_scatter(n, weighted):
            nc.vector.tensor_tensor(window(n, 0, P), weighted[:], zeros[:], ALU.add)

        def expansion(piece, n, pieces=1, home=None):
            start, width = WIDTH * piece, WIDTH * pieces
            if piece == 1 and n < 2:
                start, width = P, P + WIDTH
                y = keep.tile([P, width], F32, name=f"x0{n}")[:]
            elif home:
                y = keep.tile([P, width], F32, name=home)[:]
            elif pieces > 1:
                y = keep.tile([P, width], F32, name=f"x0{n - 4}")[:]
            else:
                if piece not in y_tiles:
                    y_tiles[piece] = keep.tile([P, NT, WIDTH], F32, name=f"raw{(piece + 2) % 4}")
                y = y_tiles[piece][:, n, :]
            nc.scalar.activation(y, second_product(n, start, width), ACT.Relu)
            nc.vector.tensor_tensor(window(n, start, width), y, weights[:, start : start + width], ALU.mult)
            if start + width == S:
                queues = (nc.sync, nc.scalar) if n == NT - 1 else (nc.sync,)
                for i, queue in enumerate(queues):
                    cols = slice(i * T2 // len(queues), (i + 1) * T2 // len(queues))
                    queue.dma_start(out[P * n : P * (n + 1), cols], cache[n][:, cols])

        def halves_of(name):
            both = keep.tile([P, 2, BANK], F32, name=name)
            return [both[:, i] for i in range(2)]

        gather_words(0)
        nc.vector.tensor_copy(v_s[:], tab_s[:].bitcast(U8).indirect(picks[:]))
        early = [bank(i) for i in range(2)]
        second_pair = [bank(i) for i in (2, 3)]
        ahead = [bank(i) for i in (6, 7)]
        for a in range(KA):
            quantise_w1(0, a, [("scalar", 0, P)], PASS)
            if a > 0:
                gather_words(a)
            for u in range(2):
                first_passes(early[u], 0, a, u)
            pair_passes(second_pair, 0, 1, a, a == 0, a == KA - 1)
            pair_passes(ahead, 0, 2, a, a == 0, a == KA - 1)

        x0 = [woven_relu(early[u], f"x0{u}") for u in range(2)]
        for u in range(2):
            woven_log(x0[u])

        lead = [bank(4 + u) for u in range(2)]
        for a in range(KA - 1):
            quantise_w1(1, a, [("vector", 0, P)], PASS)
            for u in range(2):
                first_passes(lead[u], 1, a, u)
        quantise_w1(1, KA - 1, [("vector", 0, P)], 2 * P)
        first_passes(lead[0], 1, KA - 1, 0)
        first_passes(lead[1], 1, KA - 1, 1, (3, 2, 1, 0))
        halves = [slice(c0, c0 + P // 2) for c0 in (0, P // 2)]
        x1 = [keep.tile([P, P, PACK], F32, name=f"x1{u}") for u in range(2)]
        cut = [x1[0], keep.tile([P, P, PACK], F32, name="lead_cut")]
        for u in range(2):
            for half in halves:
                nc.scalar.activation(
                    cut[u][:, half], lead[u][:].rearrange("p (t c) -> p c t", t=PACK)[:, half], ACT.Relu
                )
            for half in halves:
                plane_log(x1[u][:, half], cut[u][:, half])
        x01 = halves_of("second")
        for i in range(2):
            plane_relu(second_pair[i], x01[i])
        for x in x01:
            plane_log(x, x)
        planes = plane_gains(x01, 0, 1)
        x02 = [keep.tile([P, BANK], F32, name="ahead")[:], keep.tile([P, BANK], F32, name="lead_cut")[:]]
        early_feat = stage.tile([P, 2 * PASS], BF16, name="feat", align_bytes=64)
        interleave(early_feat, planes)
        plane_relu(ahead[0], x02[0])
        feat = shared.tile([P, 2, P, PACK], BF16, name="opening_feat", align_bytes=64, offset=0)
        for u in range(2):
            nc.vector.tensor_tensor(feat[:, u], x0[u], gain_rows[0][:], ALU.mult)
        first = keep.tile([P, P, PACK], BF16, name="feat1w0", align_bytes=64)
        for half in halves:
            nc.vector.tensor_tensor(first[:, half], x1[0][:, half], gain_rows[1][:, half], ALU.mult)
        quantise_h(feat[:, 0:2].rearrange("p u c t -> p (u c t)"), 0, 0, 2 * P)
        quantise_h(first[:].rearrange("p c t -> p (c t)"), 1, 0, P)
        second = keep.tile([P, P, PACK], BF16, name="feat1w1", align_bytes=64)
        for half in halves:
            nc.vector.tensor_tensor(second[:, half], x1[1][:, half], gain_rows[1][:, half], ALU.mult)
        weighted = [opening_product(0, "weighted0")]
        quantise_h(second[:].rearrange("p c t -> p (c t)"), 1, P, 2 * P)
        weighted.append(opening_product(1, "weighted1"))
        for n in range(2):
            opening_scatter(n, weighted[n])
        quantise_h(early_feat[:], 0, WIDTH, 2 * WIDTH)
        sums = pair_product(1, 1, [0, 1], (0, 1, 2))
        x11 = halves_of("x10")
        for i in range(2):
            plane_relu(sums[i], x11[i])
        expansion(0, 2)
        expansion(0, 3)
        for x in x11:
            plane_log(x, x)
        plane_relu(ahead[1], x02[1])
        expansion(0, 4)
        planes = plane_gains(x11, 1, 1)
        logs = halves_of("x11")
        plane_log(logs[0], x02[0])
        f11 = weave(planes, 1, 1)
        expansion(0, 5)
        plane_log(logs[1], x02[1])
        planes = plane_gains(logs, 0, 2)
        expansion(1, 0)
        f02 = weave(planes, 0, 2)
        expansion(1, 1)

        sums = pair_product(1, 2, [6, 7], (2, 0, 1))
        x12 = halves_of("ahead")
        for i in range(2):
            plane_relu(sums[i], x12[i])
        expansion(1, 2)
        for x in x12:
            plane_log(x, x)
        planes = plane_gains(x12, 1, 2)
        expansion(1, 3)
        f12 = weave(planes, 1, 2)

        sums = pair_product(0, 3, [2, 3], (0, 1, 2))
        x03 = halves_of("x10")
        for i in range(2):
            plane_relu(sums[i], x03[i])
            expansion(1, 4 + i)
        for x in x03:
            plane_log(x, x)
        planes = plane_gains(x03, 0, 3)
        expansion(2, 0)
        f03 = weave(planes, 0, 3)
        sums = pair_product(1, 3, [6, 7], (0, 1, 2))
        x13 = halves_of("x11")
        for i in range(2):
            plane_relu(sums[i], x13[i])
        expansion(2, 1)
        for x in x13:
            plane_log(x, x)
        planes = plane_gains(x13, 1, 3)
        expansion(2, 2)
        f13 = weave(planes, 1, 3)
        expansion(2, 3, home="planes1")
        for n in range(4):
            expansion(3, n)
        for n in range(4, NT):
            expansion(2, n, pieces=2)
